import numpy as np
import ml_dtypes


def mxq(x, axis, fmt="e4m3"):
    dtype, down = {"e4m3": (ml_dtypes.float8_e4m3fn, 7), "e5m2": (ml_dtypes.float8_e5m2, 14)}[fmt]
    v = np.moveaxis(np.asarray(x, np.float32).astype(ml_dtypes.bfloat16).astype(np.float64), axis, -1)
    blocks = v.reshape(v.shape[:-1] + (-1, 32))
    amax = np.abs(blocks).max(-1, keepdims=True)
    byte = np.maximum(np.where(amax > 0, np.frexp(amax)[1] - 1 + 127, 0) - down, 1)
    scale = np.exp2(byte - 127.0)
    codes = (blocks / scale).astype(np.float32).astype(dtype).astype(np.float64)
    return np.moveaxis((codes * scale).reshape(v.shape), -1, axis)


WIDE = False


def mx_kscale(k):
    if not WIDE:
        return np.ones(k)
    levels = np.array([10, -10, 5, -5, 0])
    if k % 512:
        return np.exp2(np.random.permutation(np.resize(levels, k // 32))).repeat(32)
    a = np.empty((k // 512, 16))
    for p in range(k // 512):
        a[p, :8] = np.random.permutation(np.resize(levels, 8))
        for g in range(8):
            far = levels[np.abs(levels - a[p, g]) >= 10]
            a[p, g + 8] = far[np.random.randint(len(far))]
    return np.exp2(a.ravel()).repeat(32)


def f64(x):
    return np.asarray(x).astype(np.float64)


def striped8(idx):
    return np.concatenate([x.reshape(-1, 16).T for x in idx]).astype(np.uint16)


def runs(offs, k):
    lists = np.stack([offs[16 * r : 16 * r + 16].T.reshape(-1) for r in range(8)]).astype(np.int64)
    return lists[np.arange(k) % 512 // 64]


def pack_weight(w):
    k, n = w.shape
    w = f64(np.asarray(w, np.float32).astype(ml_dtypes.bfloat16)).reshape(k // 32, 32, n)
    amax = np.abs(w).max(1)
    byte = np.clip(np.where(amax > 0, np.frexp(amax)[1] - 1 + 127 - 7, 1), 1, 254)
    scaled = (w * np.exp2(127.0 - byte)[:, None, :]).reshape(k, n).astype(np.float32)
    words = np.ascontiguousarray(scaled.reshape(k // 512, 128, 4, n).transpose(0, 1, 3, 2)).astype(ml_dtypes.float8_e4m3fn).view(np.uint8)
    return words, np.ascontiguousarray(byte.astype(np.uint8).reshape(k // 512, 16, n))


def unpack_weight(words, scales):
    g, p, n, _ = words.shape
    vals = np.ascontiguousarray(words).view(ml_dtypes.float8_e4m3fn).astype(np.float64) * np.repeat(np.exp2(scales.astype(np.float64) - 127.0), 8, axis=1)[..., None]
    return vals.transpose(0, 1, 3, 2).reshape(g * 512, n)


def gelu(v):
    return 0.5 * v * (1.0 + np.tanh(np.sqrt(2.0 / np.pi) * (v + 0.044715 * v**3)))


K, T, S, N = 512, 2048, 1024, 256


def setup_inputs():
    n = np.random.standard_normal
    s = mx_kscale(K)[:, None]
    packed_xT = pack_weight(n((K, T)) * s)
    return {
        "x_words": packed_xT[0],
        "x_scales": packed_xT[1],
        "w1": (n((K, N)) / np.sqrt(K) / s).astype(np.float32),
        "w2": (n((K, N)) / np.sqrt(K) / s).astype(np.float32),
        "offs": striped8(np.stack([np.random.permutation(T)[:S] for _ in range(8)])),
    }


def reference(x_words, x_scales, w1, w2, offs):
    xq = unpack_weight(x_words, x_scales)[np.arange(K)[:, None], runs(offs, K)]
    return (gelu(mxq(f64(w1), 0, "e4m3").T @ xq)) * ((mxq(f64(w2), 0, "e4m3").T @ xq))

@@ -1,0 +1,115 @@
+from contextlib import ExitStack
+
+import concourse.mybir as mybir
+
+K, T, S, N = 512, 2048, 1024, 256
+FLOPS = 2 * 2 * K * N * S
+
+F32 = mybir.dt.float32
+BF16 = mybir.dt.bfloat16
+I32 = mybir.dt.int32
+U32 = mybir.dt.uint32
+U16 = mybir.dt.uint16
+U8 = mybir.dt.uint8
+FP8X4 = mybir.dt.float8_e4m3fn_x4
+GELU = mybir.ActivationFunctionType.Gelu_apprx_tanh
+MULT = mybir.AluOpType.mult
+
+P = 128
+PACK = 4
+M_TILE = 128
+N_TILE = 512
+
+
+def tile_picked_phglu_gelu_p_kernel(tc, x_words, x_scales, w1, w2, offs, out):
+    nc = tc.nc
+    with ExitStack() as ctx:
+        keep = ctx.enter_context(tc.tile_pool(name="keep", bufs=1))
+        psum = ctx.enter_context(tc.psum_pool(name="psum", bufs=1))
+
+        offsets = keep.tile([P, S // 16], U16, name="offsets")
+        nc.sync.dma_start(offsets[:], offs)
+
+        scale_table = keep.tile([P, T], U8, name="scale_table", align_bytes=64)
+        nc.vector.memset(scale_table[:].bitcast(I32), 0)
+        nc.sync.dma_start(scale_table[0:P:8, :].bitcast(I32), x_scales[0].bitcast(I32))
+
+        raw = {}
+
+        def load_w(m):
+            for a, w in enumerate((w1, w2)):
+                t = keep.tile([P, PACK, M_TILE], F32, name=f"raw{m}{a}")
+                nc.scalar.dma_start(t[:], w[:, m * M_TILE : (m + 1) * M_TILE].rearrange("(p j) c -> p j c", j=PACK))
+                raw[m, a] = t
+
+        load_w(0)
+        word_table = keep.tile([P, T], U32, name="word_table", align_bytes=64)
+        nc.scalar.dma_start(word_table[:].bitcast(I32), x_words[0].rearrange("p c r -> p (c r)").bitcast(I32))
+        load_w(1)
+
+        x_plane = keep.tile([P, S], U8, name="x_plane", align_bytes=64)
+        nc.gpsimd.memset(x_plane[:].bitcast(I32), 0)
+
+        warm = keep.tile([P, 2], F32, name="warm")
+        nc.gpsimd.memset(warm[:, 0:1], 0.0)
+        nc.scalar.activation(warm[:, 1:2], warm[:, 0:1], GELU)
+
+        picked_scales = keep.tile([P, S], U8, name="picked_scales", align_bytes=64)
+        nc.vector.tensor_copy(picked_scales[:], scale_table[:].indirect(offsets[:]))
+        for i in range(4):
+            nc.sync.dma_start(x_plane[i:P:32, :].bitcast(I32), picked_scales[8 * i : P : 32, :].bitcast(I32))
+
+        codes = {}
+
+        def quantize_w(m):
+            grouped = keep.tile([P, 2, M_TILE, PACK], BF16, name=f"grouped{m}", align_bytes=64)
+            for a in range(2):
+                nc.scalar.copy(grouped[:, a], raw[m, a][:].rearrange("p j c -> p c j"))
+            w_words = keep.tile([P, 2 * M_TILE], U32, name=f"w_words{m}", align_bytes=64)
+            w_plane = keep.tile([P, 2 * M_TILE], U8, name=f"w_plane{m}", align_bytes=64)
+            nc.vector.quantize_mx(
+                out=w_words[:].bitcast(FP8X4), scales=w_plane[:], in_=grouped[:].rearrange("p a c j -> p (a c j)")
+            )
+            codes[m] = (w_words, w_plane)
+
+        picked = {}
+
+        def gather(h):
+            t = keep.tile([P, N_TILE], U32, name=f"picked{h}", align_bytes=64)
+            nc.vector.tensor_copy(t[:], word_table[:].indirect(offsets[:, h * 32 : (h + 1) * 32]))
+            picked[h] = t
+
+        def block(m, h, pieces):
+            w_words, w_plane = codes[m]
+            acc = []
+            for a in range(2):
+                bank = psum.tile([P, N_TILE], F32, name=f"bank{m}{h}{a}")
+                cols = slice(a * M_TILE, (a + 1) * M_TILE)
+                nc.tensor.matmul_mx(
+                    out=bank[:],
+                    lhsT=w_words[:, cols].bitcast(FP8X4),
+                    lhsT_scale=w_plane[:, cols],
+                    rhs=picked[h][:].bitcast(FP8X4),
+                    rhs_scale=x_plane[:, h * N_TILE : (h + 1) * N_TILE],
+                    start=True,
+                    stop=True,
+                )
+                acc.append(bank)
+            gate = keep.tile([P, N_TILE], F32, name=f"gate{m}{h}")
+            nc.scalar.activation(gate[:], acc[0][:], GELU)
+            width = N_TILE // pieces
+            for c in range(pieces):
+                cols = slice(c * width, (c + 1) * width)
+                res = keep.tile([P, width], F32, name=f"res{m}{h}{c}")
+                nc.vector.tensor_tensor(res[:], gate[:, cols], acc[1][:, cols], MULT)
+                j0 = h * N_TILE + c * width
+                nc.sync.dma_start(out[m * M_TILE : (m + 1) * M_TILE, j0 : j0 + width], res[:])
+
+        quantize_w(0)
+        gather(0)
+        gather(1)
+        block(0, 0, 1)
+        quantize_w(1)
+        block(0, 1, 1)
+        block(1, 0, 1)
+        block(1, 1, 2)

@@ -36,33 +36,38 @@ def tile_picked_phglu_gelu_p_kernel(tc, x_words, x_scales, w1, w2, offs, out):
 
         raw = {}
 
-        def load_w(m):
+        def load_w(m, queue):
             for a, w in enumerate((w1, w2)):
                 t = keep.tile([P, PACK, M_TILE], F32, name=f"raw{m}{a}")
-                nc.scalar.dma_start(t[:], w[:, m * M_TILE : (m + 1) * M_TILE].rearrange("(p j) c -> p j c", j=PACK))
+                queue.dma_start(t[:], w[:, m * M_TILE : (m + 1) * M_TILE].rearrange("(p j) c -> p j c", j=PACK))
                 raw[m, a] = t
 
-        load_w(0)
+        load_w(0, nc.sync)
         word_table = keep.tile([P, T], U32, name="word_table", align_bytes=64)
-        nc.scalar.dma_start(word_table[:].bitcast(I32), x_words[0].rearrange("p c r -> p (c r)").bitcast(I32))
-        load_w(1)
+        nc.sync.dma_start(word_table[:].bitcast(I32), x_words[0].rearrange("p c r -> p (c r)").bitcast(I32))
+        load_w(1, nc.sync)
 
-        x_plane = keep.tile([P, S], U8, name="x_plane", align_bytes=64)
-        nc.gpsimd.memset(x_plane[:].bitcast(I32), 0)
+        x_plane = []
+        for h in range(2):
+            plane = keep.tile([P, N_TILE], U8, name=f"x_plane{h}", align_bytes=64)
+            nc.gpsimd.memset(plane[:].bitcast(I32), 0)
+            x_plane.append(plane)
 
         warm = keep.tile([P, 2], F32, name="warm")
         nc.gpsimd.memset(warm[:, 0:1], 0.0)
         nc.scalar.activation(warm[:, 1:2], warm[:, 0:1], GELU)
 
-        picked_scales = keep.tile([P, S], U8, name="picked_scales", align_bytes=64)
-        nc.vector.tensor_copy(picked_scales[:], scale_table[:].indirect(offsets[:]))
-        for i in range(4):
-            nc.sync.dma_start(x_plane[i:P:32, :].bitcast(I32), picked_scales[8 * i : P : 32, :].bitcast(I32))
+        for h in range(2):
+            queue = nc.sync
+            picked_scales = keep.tile([P, N_TILE], U8, name=f"picked_scales{h}", align_bytes=64)
+            nc.vector.tensor_copy(picked_scales[:], scale_table[:].indirect(offsets[:, h * 32 : (h + 1) * 32]))
+            for i in range(4):
+                queue.dma_start(x_plane[h][i:P:32, :].bitcast(I32), picked_scales[8 * i : P : 32, :].bitcast(I32))
 
         codes = {}
 
         def quantize_w(m):
-            grouped = keep.tile([P, 2, M_TILE, PACK], BF16, name=f"grouped{m}", align_bytes=64)
+            grouped = keep.tile([P, 2, M_TILE, PACK], BF16, name=f"grouped{m}", tag=f"slot{m}", align_bytes=64)
             for a in range(2):
                 nc.scalar.copy(grouped[:, a], raw[m, a][:].rearrange("p j c -> p c j"))
             w_words = keep.tile([P, 2 * M_TILE], U32, name=f"w_words{m}", align_bytes=64)
@@ -75,22 +80,41 @@ def tile_picked_phglu_gelu_p_kernel(tc, x_words, x_scales, w1, w2, offs, out):
         picked = {}
 
         def gather(h):
-            t = keep.tile([P, N_TILE], U32, name=f"picked{h}", align_bytes=64)
+            t = keep.tile([P, N_TILE], U32, name=f"picked{h}", tag=f"slot{2 * h}", align_bytes=64)
             nc.vector.tensor_copy(t[:], word_table[:].indirect(offsets[:, h * 32 : (h + 1) * 32]))
             picked[h] = t
+
+        banks = {}
+        for m in range(2):
+            for h in range(2):
+                for a in range(2):
+                    banks[m, h, a] = psum.tile([P, N_TILE], F32, name=f"bank{m}{h}{a}")
+
+        def warm_up():
+            w_words, w_plane = codes[0]
+            for r in range(4):
+                nc.tensor.matmul_mx(
+                    out=banks[1, 1, r // 2][:, (r % 2) * 256 : (r % 2 + 1) * 256],
+                    lhsT=w_words[:, 0:M_TILE].bitcast(FP8X4),
+                    lhsT_scale=w_plane[:, 0:M_TILE],
+                    rhs=w_words[:].bitcast(FP8X4),
+                    rhs_scale=w_plane[:],
+                    start=True,
+                    stop=True,
+                )
 
         def block(m, h, pieces):
             w_words, w_plane = codes[m]
             acc = []
             for a in range(2):
-                bank = psum.tile([P, N_TILE], F32, name=f"bank{m}{h}{a}")
+                bank = banks[m, h, a]
                 cols = slice(a * M_TILE, (a + 1) * M_TILE)
                 nc.tensor.matmul_mx(
                     out=bank[:],
                     lhsT=w_words[:, cols].bitcast(FP8X4),
                     lhsT_scale=w_plane[:, cols],
                     rhs=picked[h][:].bitcast(FP8X4),
-                    rhs_scale=x_plane[:, h * N_TILE : (h + 1) * N_TILE],
+                    rhs_scale=x_plane[h][:],
                     start=True,
                     stop=True,
                 )
@@ -106,10 +130,11 @@ def tile_picked_phglu_gelu_p_kernel(tc, x_words, x_scales, w1, w2, offs, out):
                 nc.sync.dma_start(out[m * M_TILE : (m + 1) * M_TILE, j0 : j0 + width], res[:])
 
         quantize_w(0)
+        warm_up()
         gather(0)
         gather(1)
-        block(0, 0, 1)
         quantize_w(1)
-        block(0, 1, 1)
+        block(0, 0, 1)
         block(1, 0, 1)
+        block(0, 1, 1)
         block(1, 1, 2)

@@ -26,26 +26,29 @@ def tile_picked_phglu_gelu_p_kernel(tc, x_words, x_scales, w1, w2, offs, out):
     with ExitStack() as ctx:
         keep = ctx.enter_context(tc.tile_pool(name="keep", bufs=1))
         psum = ctx.enter_context(tc.psum_pool(name="psum", bufs=1))
+        weights = (w1, w2)
 
         offsets = keep.tile([P, S // 16], U16, name="offsets")
         nc.sync.dma_start(offsets[:], offs)
 
         scale_table = keep.tile([P, T], U8, name="scale_table", align_bytes=64)
-        nc.vector.memset(scale_table[:].bitcast(I32), 0)
-        nc.sync.dma_start(scale_table[0:P:8, :].bitcast(I32), x_scales[0].bitcast(I32))
+        nc.vector.memset(scale_table[:, 0 : T // 2].bitcast(I32), 0)
+        nc.gpsimd.memset(scale_table[:, T // 2 : T].bitcast(I32), 0)
 
         raw = {}
 
-        def load_w(m, queue):
-            for a, w in enumerate((w1, w2)):
-                t = keep.tile([P, PACK, M_TILE], F32, name=f"raw{m}{a}")
-                queue.dma_start(t[:], w[:, m * M_TILE : (m + 1) * M_TILE].rearrange("(p j) c -> p j c", j=PACK))
-                raw[m, a] = t
+        def load_w(m, a):
+            t = keep.tile([P, PACK, M_TILE], F32, name=f"raw{m}{a}", tag=f"raw{m}{a}")
+            nc.sync.dma_start(t[:], weights[a][:, m * M_TILE : (m + 1) * M_TILE].rearrange("(p j) c -> p j c", j=PACK))
+            raw[m, a] = t
 
-        load_w(0, nc.sync)
+        load_w(0, 0)
+        nc.sync.dma_start(scale_table[0:P:8, :].bitcast(I32), x_scales[0].bitcast(I32))
+        load_w(0, 1)
         word_table = keep.tile([P, T], U32, name="word_table", align_bytes=64)
         nc.sync.dma_start(word_table[:].bitcast(I32), x_words[0].rearrange("p c r -> p (c r)").bitcast(I32))
-        load_w(1, nc.sync)
+        load_w(1, 0)
+        load_w(1, 1)
 
         x_plane = []
         for h in range(2):
@@ -57,19 +60,24 @@ def tile_picked_phglu_gelu_p_kernel(tc, x_words, x_scales, w1, w2, offs, out):
         nc.gpsimd.memset(warm[:, 0:1], 0.0)
         nc.scalar.activation(warm[:, 1:2], warm[:, 0:1], GELU)
 
-        for h in range(2):
-            queue = nc.sync
+        def scales(h):
             picked_scales = keep.tile([P, N_TILE], U8, name=f"picked_scales{h}", align_bytes=64)
             nc.vector.tensor_copy(picked_scales[:], scale_table[:].indirect(offsets[:, h * 32 : (h + 1) * 32]))
             for i in range(4):
-                queue.dma_start(x_plane[h][i:P:32, :].bitcast(I32), picked_scales[8 * i : P : 32, :].bitcast(I32))
+                nc.sync.dma_start(x_plane[h][i:P:32, :].bitcast(I32), picked_scales[8 * i : P : 32, :].bitcast(I32))
+
+        scales(0)
+        scales(1)
 
         codes = {}
 
         def quantize_w(m):
             grouped = keep.tile([P, 2, M_TILE, PACK], BF16, name=f"grouped{m}", tag=f"slot{m}", align_bytes=64)
             for a in range(2):
-                nc.scalar.copy(grouped[:, a], raw[m, a][:].rearrange("p j c -> p c j"))
+                nc.scalar.copy(
+                    grouped[:, a].rearrange("p (c i) j -> p c j i", i=4),
+                    raw[m, a][:].rearrange("p j (c i) -> p c j i", i=4),
+                )
             w_words = keep.tile([P, 2 * M_TILE], U32, name=f"w_words{m}", align_bytes=64)
             w_plane = keep.tile([P, 2 * M_TILE], U8, name=f"w_plane{m}", align_bytes=64)
             nc.vector.quantize_mx(
@@ -77,12 +85,13 @@ def tile_picked_phglu_gelu_p_kernel(tc, x_words, x_scales, w1, w2, offs, out):
             )
             codes[m] = (w_words, w_plane)
 
-        picked = {}
+        picked = {0: [], 1: []}
 
-        def gather(h):
-            t = keep.tile([P, N_TILE], U32, name=f"picked{h}", tag=f"slot{2 * h}", align_bytes=64)
-            nc.vector.tensor_copy(t[:], word_table[:].indirect(offsets[:, h * 32 : (h + 1) * 32]))
-            picked[h] = t
+        def gather(h, j0, width, tag):
+            t = keep.tile([P, width], U32, name=f"picked{h}{j0}", tag=tag, align_bytes=64)
+            c0 = (h * N_TILE + j0) // 16
+            nc.vector.tensor_copy(t[:], word_table[:].indirect(offsets[:, c0 : c0 + width // 16]))
+            picked[h].append((t, slice(j0, j0 + width)))
 
         banks = {}
         for m in range(2):
@@ -103,38 +112,39 @@ def tile_picked_phglu_gelu_p_kernel(tc, x_words, x_scales, w1, w2, offs, out):
                     stop=True,
                 )
 
-        def block(m, h, pieces):
+        def product(m, h, a):
             w_words, w_plane = codes[m]
-            acc = []
-            for a in range(2):
-                bank = banks[m, h, a]
-                cols = slice(a * M_TILE, (a + 1) * M_TILE)
+            w_cols = slice(a * M_TILE, (a + 1) * M_TILE)
+            for t, cols in picked[h]:
                 nc.tensor.matmul_mx(
-                    out=bank[:],
-                    lhsT=w_words[:, cols].bitcast(FP8X4),
-                    lhsT_scale=w_plane[:, cols],
-                    rhs=picked[h][:].bitcast(FP8X4),
-                    rhs_scale=x_plane[h][:],
+                    out=banks[m, h, a][:, cols],
+                    lhsT=w_words[:, w_cols].bitcast(FP8X4),
+                    lhsT_scale=w_plane[:, w_cols],
+                    rhs=t[:].bitcast(FP8X4),
+                    rhs_scale=x_plane[h][:, cols],
                     start=True,
                     stop=True,
                 )
-                acc.append(bank)
-            gate = keep.tile([P, N_TILE], F32, name=f"gate{m}{h}")
-            nc.scalar.activation(gate[:], acc[0][:], GELU)
+
+        def finish(m, h, pieces, tag):
+            gate = keep.tile([P, N_TILE], F32, name=f"gate{m}{h}", tag=tag)
             width = N_TILE // pieces
             for c in range(pieces):
                 cols = slice(c * width, (c + 1) * width)
+                nc.scalar.activation(gate[:, cols], banks[m, h, 0][:, cols], GELU)
                 res = keep.tile([P, width], F32, name=f"res{m}{h}{c}")
-                nc.vector.tensor_tensor(res[:], gate[:, cols], acc[1][:, cols], MULT)
+                nc.vector.tensor_tensor(res[:], gate[:, cols], banks[m, h, 1][:, cols], MULT)
                 j0 = h * N_TILE + c * width
                 nc.sync.dma_start(out[m * M_TILE : (m + 1) * M_TILE, j0 : j0 + width], res[:])
 
         quantize_w(0)
         warm_up()
-        gather(0)
-        gather(1)
+        gather(0, 0, 512, "slot0")
+        gather(1, 0, 256, "picked10")
         quantize_w(1)
-        block(0, 0, 1)
-        block(1, 0, 1)
-        block(0, 1, 1)
-        block(1, 1, 2)
+        gather(1, 256, 256, "slot1")
+        for h in range(2):
+            for m in range(2):
+                product(m, h, 0)
+                product(m, h, 1)
+                finish(m, h, 2 if m + h == 2 else 1, f"gate{m}{h}")

@@ -32,66 +32,69 @@ def tile_picked_phglu_gelu_p_kernel(tc, x_words, x_scales, w1, w2, offs, out):
         nc.sync.dma_start(offsets[:], offs)
 
         scale_table = keep.tile([P, T], U8, name="scale_table", align_bytes=64)
-        nc.vector.memset(scale_table[:, 0 : T // 2].bitcast(I32), 0)
-        nc.gpsimd.memset(scale_table[:, T // 2 : T].bitcast(I32), 0)
-
+        nc.vector.memset(scale_table[:].bitcast(I32), 0)
+        word_table = keep.tile([P, T], U32, name="word_table", tag="word_table", align_bytes=64)
         raw = {}
 
-        def load_w(m, a):
-            t = keep.tile([P, PACK, M_TILE], F32, name=f"raw{m}{a}", tag=f"raw{m}{a}")
+        def load_scales():
+            nc.sync.dma_start(scale_table[0:P:8, :].bitcast(I32), x_scales[0].bitcast(I32))
+
+        def load_words():
+            nc.sync.dma_start(word_table[:].bitcast(I32), x_words[0].rearrange("p c r -> p (c r)").bitcast(I32))
+
+        def load_w(m, a, tag=None):
+            t = keep.tile([P, PACK, M_TILE], F32, name=f"raw{m}{a}", tag=tag or f"raw{m}{a}", align_bytes=64)
             nc.sync.dma_start(t[:], weights[a][:, m * M_TILE : (m + 1) * M_TILE].rearrange("(p j) c -> p j c", j=PACK))
             raw[m, a] = t
 
-        load_w(0, 0)
-        nc.sync.dma_start(scale_table[0:P:8, :].bitcast(I32), x_scales[0].bitcast(I32))
-        load_w(0, 1)
-        word_table = keep.tile([P, T], U32, name="word_table", align_bytes=64)
-        nc.sync.dma_start(word_table[:].bitcast(I32), x_words[0].rearrange("p c r -> p (c r)").bitcast(I32))
-        load_w(1, 0)
-        load_w(1, 1)
+        planes = []
 
-        x_plane = []
-        for h in range(2):
-            plane = keep.tile([P, N_TILE], U8, name=f"x_plane{h}", align_bytes=64)
-            nc.gpsimd.memset(plane[:].bitcast(I32), 0)
-            x_plane.append(plane)
-
-        warm = keep.tile([P, 2], F32, name="warm")
-        nc.gpsimd.memset(warm[:, 0:1], 0.0)
-        nc.scalar.activation(warm[:, 1:2], warm[:, 0:1], GELU)
-
-        def scales(h):
-            picked_scales = keep.tile([P, N_TILE], U8, name=f"picked_scales{h}", align_bytes=64)
-            nc.vector.tensor_copy(picked_scales[:], scale_table[:].indirect(offsets[:, h * 32 : (h + 1) * 32]))
+        def scales(j0, width):
+            plane = keep.tile([P, width], U8, name=f"x_plane{j0}", align_bytes=64)
+            nc.vector.memset(plane[:].bitcast(I32), 0)
+            picked_scales = keep.tile([P, width], U8, name=f"picked_scales{j0}", tag=f"picked_scales{j0}", align_bytes=64)
+            nc.vector.tensor_copy(picked_scales[:], scale_table[:].indirect(offsets[:, j0 // 16 : (j0 + width) // 16]))
             for i in range(4):
-                nc.sync.dma_start(x_plane[h][i:P:32, :].bitcast(I32), picked_scales[8 * i : P : 32, :].bitcast(I32))
+                nc.sync.dma_start(plane[i:P:32, :].bitcast(I32), picked_scales[8 * i : P : 32, :].bitcast(I32))
+            planes.append((plane, j0, width))
 
-        scales(0)
-        scales(1)
+        def plane_of(j0, width):
+            for plane, p0, pw in planes:
+                if p0 <= j0 and j0 + width <= p0 + pw:
+                    return plane[:, j0 - p0 : j0 - p0 + width]
+
+        def warm_table():
+            warm = keep.tile([P, 2], F32, name="warm")
+            nc.gpsimd.memset(warm[:, 0:1], 0.0)
+            nc.scalar.activation(warm[:, 1:2], warm[:, 0:1], GELU)
 
         codes = {}
+        whole = {}
 
-        def quantize_w(m):
-            grouped = keep.tile([P, 2, M_TILE, PACK], BF16, name=f"grouped{m}", tag=f"slot{m}", align_bytes=64)
-            for a in range(2):
-                nc.scalar.copy(
-                    grouped[:, a].rearrange("p (c i) j -> p c j i", i=4),
-                    raw[m, a][:].rearrange("p j (c i) -> p c j i", i=4),
+        def quantize_w(pieces, tag, words_tag=None, cast=nc.scalar.copy):
+            n = len(pieces)
+            grouped = keep.tile([P, n, M_TILE, PACK], BF16, name=f"grouped{tag}", tag=tag, align_bytes=64)
+            for i, piece in enumerate(pieces):
+                cast(
+                    grouped[:, i].rearrange("p (c i) j -> p c j i", i=4),
+                    raw[piece][:].rearrange("p j (c i) -> p c j i", i=4),
                 )
-            w_words = keep.tile([P, 2 * M_TILE], U32, name=f"w_words{m}", align_bytes=64)
-            w_plane = keep.tile([P, 2 * M_TILE], U8, name=f"w_plane{m}", align_bytes=64)
+            w_words = keep.tile([P, n * M_TILE], U32, name=f"w_words{tag}", tag=words_tag or f"w_words{tag}", align_bytes=64)
+            w_plane = keep.tile([P, n * M_TILE], U8, name=f"w_plane{tag}", align_bytes=64)
             nc.vector.quantize_mx(
                 out=w_words[:].bitcast(FP8X4), scales=w_plane[:], in_=grouped[:].rearrange("p a c j -> p (a c j)")
             )
-            codes[m] = (w_words, w_plane)
+            whole[tag] = (w_words[:].bitcast(FP8X4), w_plane[:])
+            for i, piece in enumerate(pieces):
+                cols = slice(i * M_TILE, (i + 1) * M_TILE)
+                codes[piece] = (w_words[:, cols].bitcast(FP8X4), w_plane[:, cols])
 
-        picked = {0: [], 1: []}
+        picked = []
 
-        def gather(h, j0, width, tag):
-            t = keep.tile([P, width], U32, name=f"picked{h}{j0}", tag=tag, align_bytes=64)
-            c0 = (h * N_TILE + j0) // 16
-            nc.vector.tensor_copy(t[:], word_table[:].indirect(offsets[:, c0 : c0 + width // 16]))
-            picked[h].append((t, slice(j0, j0 + width)))
+        def gather(j0, width, tag):
+            t = keep.tile([P, width], U32, name=f"picked{j0}", tag=tag, align_bytes=64)
+            nc.vector.tensor_copy(t[:], word_table[:].indirect(offsets[:, j0 // 16 : (j0 + width) // 16]))
+            picked.append((t, j0, width))
 
         banks = {}
         for m in range(2):
@@ -100,51 +103,67 @@ def tile_picked_phglu_gelu_p_kernel(tc, x_words, x_scales, w1, w2, offs, out):
                     banks[m, h, a] = psum.tile([P, N_TILE], F32, name=f"bank{m}{h}{a}")
 
         def warm_up():
-            w_words, w_plane = codes[0]
-            for r in range(4):
+            w_words, w_plane = codes[0, 0]
+            for r in range(8):
                 nc.tensor.matmul_mx(
-                    out=banks[1, 1, r // 2][:, (r % 2) * 256 : (r % 2 + 1) * 256],
-                    lhsT=w_words[:, 0:M_TILE].bitcast(FP8X4),
-                    lhsT_scale=w_plane[:, 0:M_TILE],
-                    rhs=w_words[:].bitcast(FP8X4),
-                    rhs_scale=w_plane[:],
+                    out=banks[1, 1, r // 4][:, (r % 4) * 128 : (r % 4 + 1) * 128],
+                    lhsT=w_words,
+                    lhsT_scale=w_plane,
+                    rhs=w_words,
+                    rhs_scale=w_plane,
                     start=True,
                     stop=True,
                 )
 
         def product(m, h, a):
-            w_words, w_plane = codes[m]
-            w_cols = slice(a * M_TILE, (a + 1) * M_TILE)
-            for t, cols in picked[h]:
-                nc.tensor.matmul_mx(
-                    out=banks[m, h, a][:, cols],
-                    lhsT=w_words[:, w_cols].bitcast(FP8X4),
-                    lhsT_scale=w_plane[:, w_cols],
-                    rhs=t[:].bitcast(FP8X4),
-                    rhs_scale=x_plane[h][:, cols],
-                    start=True,
-                    stop=True,
-                )
+            w_words, w_plane = codes[m, a]
+            for t, j0, width in picked:
+                if j0 // N_TILE == h:
+                    nc.tensor.matmul_mx(
+                        out=banks[m, h, a][:, j0 % N_TILE : j0 % N_TILE + width],
+                        lhsT=w_words,
+                        lhsT_scale=w_plane,
+                        rhs=t[:].bitcast(FP8X4),
+                        rhs_scale=plane_of(j0, width),
+                        start=True,
+                        stop=True,
+                    )
 
-        def finish(m, h, pieces, tag):
+        def finish(m, h, widths, tag):
             gate = keep.tile([P, N_TILE], F32, name=f"gate{m}{h}", tag=tag)
-            width = N_TILE // pieces
-            for c in range(pieces):
-                cols = slice(c * width, (c + 1) * width)
+            c0 = 0
+            for width in widths:
+                cols = slice(c0, c0 + width)
                 nc.scalar.activation(gate[:, cols], banks[m, h, 0][:, cols], GELU)
-                res = keep.tile([P, width], F32, name=f"res{m}{h}{c}")
+                res = keep.tile([P, width], F32, name=f"res{m}{h}{c0}")
                 nc.vector.tensor_tensor(res[:], gate[:, cols], banks[m, h, 1][:, cols], MULT)
-                j0 = h * N_TILE + c * width
+                j0 = h * N_TILE + c0
                 nc.sync.dma_start(out[m * M_TILE : (m + 1) * M_TILE, j0 : j0 + width], res[:])
+                c0 = c0 + width
 
-        quantize_w(0)
+        load_w(0, 0)
+        load_scales()
+        load_words()
+        load_w(0, 1)
+        load_w(1, 0)
+        warm_table()
+        scales(0, 1024)
+        quantize_w([(0, 0)], "q00")
+        load_w(1, 1, "q00")
         warm_up()
-        gather(0, 0, 512, "slot0")
-        gather(1, 0, 256, "picked10")
-        quantize_w(1)
-        gather(1, 256, 256, "slot1")
-        for h in range(2):
-            for m in range(2):
-                product(m, h, 0)
-                product(m, h, 1)
-                finish(m, h, 2 if m + h == 2 else 1, f"gate{m}{h}")
+        gather(0, 512, "picked0")
+        gather(512, 512, "picked512")
+        quantize_w([(0, 1), (1, 0)], "q01", "word_table")
+        quantize_w([(1, 1)], "q11", None, nc.vector.tensor_copy)
+        product(0, 0, 0)
+        product(0, 1, 0)
+        product(0, 0, 1)
+        finish(0, 0, [512], "gate00")
+        product(1, 0, 0)
+        product(0, 1, 1)
+        finish(0, 1, [512], "gate01")
+        product(1, 1, 0)
+        product(1, 0, 1)
+        finish(1, 0, [512], "gate10")
+        product(1, 1, 1)
+        finish(1, 1, [256, 256], "gate11")

@@ -39,23 +39,33 @@ def tile_picked_phglu_gelu_p_kernel(tc, x_words, x_scales, w1, w2, offs, out):
         def load_scales():
             nc.sync.dma_start(scale_table[0:P:8, :].bitcast(I32), x_scales[0].bitcast(I32))
 
-        def load_words():
-            nc.sync.dma_start(word_table[:].bitcast(I32), x_words[0].rearrange("p c r -> p (c r)").bitcast(I32))
+        def load_words(parts):
+            source = x_words[0].rearrange("p c r -> p (c r)").bitcast(I32)
+            for c0 in range(0, T, T // parts):
+                nc.sync.dma_start(word_table[:, c0 : c0 + T // parts].bitcast(I32), source[:, c0 : c0 + T // parts])
 
         def load_w(m, a, tag=None):
             t = keep.tile([P, PACK, M_TILE], F32, name=f"raw{m}{a}", tag=tag or f"raw{m}{a}", align_bytes=64)
             nc.sync.dma_start(t[:], weights[a][:, m * M_TILE : (m + 1) * M_TILE].rearrange("(p j) c -> p j c", j=PACK))
-            raw[m, a] = t
+            raw[m, a] = t[:]
 
         planes = []
+        picked_scales = {}
 
-        def scales(j0, width):
+        def gather_scales(j0, width):
+            h0 = j0 // N_TILE * N_TILE
+            if j0 == h0:
+                picked_scales[h0] = keep.tile([P, N_TILE], U8, name=f"picked_scales{h0}", align_bytes=64)
+            nc.vector.tensor_copy(
+                picked_scales[h0][:, j0 - h0 : j0 - h0 + width],
+                scale_table[:].indirect(offsets[:, j0 // 16 : (j0 + width) // 16]),
+            )
+
+        def move_scales(j0, width, queue):
             plane = keep.tile([P, width], U8, name=f"x_plane{j0}", align_bytes=64)
             nc.vector.memset(plane[:].bitcast(I32), 0)
-            picked_scales = keep.tile([P, width], U8, name=f"picked_scales{j0}", tag=f"picked_scales{j0}", align_bytes=64)
-            nc.vector.tensor_copy(picked_scales[:], scale_table[:].indirect(offsets[:, j0 // 16 : (j0 + width) // 16]))
             for i in range(4):
-                nc.sync.dma_start(plane[i:P:32, :].bitcast(I32), picked_scales[8 * i : P : 32, :].bitcast(I32))
+                queue.dma_start(plane[i:P:32, :].bitcast(I32), picked_scales[j0][8 * i : P : 32, :].bitcast(I32))
             planes.append((plane, j0, width))
 
         def plane_of(j0, width):
@@ -69,22 +79,21 @@ def tile_picked_phglu_gelu_p_kernel(tc, x_words, x_scales, w1, w2, offs, out):
             nc.scalar.activation(warm[:, 1:2], warm[:, 0:1], GELU)
 
         codes = {}
-        whole = {}
 
-        def quantize_w(pieces, tag, words_tag=None, cast=nc.scalar.copy):
+        def cast_w(piece, target):
+            nc.scalar.copy(target.rearrange("p (c i) j -> p c j i", i=4), raw[piece].rearrange("p j (c i) -> p c j i", i=4))
+
+        def quantize_w(pieces, name):
             n = len(pieces)
-            grouped = keep.tile([P, n, M_TILE, PACK], BF16, name=f"grouped{tag}", tag=tag, align_bytes=64)
+            grouped = keep.tile([P, n * M_TILE, PACK], BF16, name=f"grouped{name}", align_bytes=64)
             for i, piece in enumerate(pieces):
-                cast(
-                    grouped[:, i].rearrange("p (c i) j -> p c j i", i=4),
-                    raw[piece][:].rearrange("p j (c i) -> p c j i", i=4),
-                )
-            w_words = keep.tile([P, n * M_TILE], U32, name=f"w_words{tag}", tag=words_tag or f"w_words{tag}", align_bytes=64)
-            w_plane = keep.tile([P, n * M_TILE], U8, name=f"w_plane{tag}", align_bytes=64)
+                cast_w(piece, grouped[:, i * M_TILE : (i + 1) * M_TILE])
+            w_words = keep.tile([P, n * M_TILE], U32, name=f"w_words{name}", align_bytes=64)
+            w_plane = keep.tile([P, n * M_TILE], U8, name=f"w_plane{name}", align_bytes=64)
             nc.vector.quantize_mx(
-                out=w_words[:].bitcast(FP8X4), scales=w_plane[:], in_=grouped[:].rearrange("p a c j -> p (a c j)")
+                out=w_words[:].bitcast(FP8X4), scales=w_plane[:], in_=grouped[:].rearrange("p c j -> p (c j)")
             )
-            whole[tag] = (w_words[:].bitcast(FP8X4), w_plane[:])
+            codes[name] = (w_words[:].bitcast(FP8X4), w_plane[:])
             for i, piece in enumerate(pieces):
                 cols = slice(i * M_TILE, (i + 1) * M_TILE)
                 codes[piece] = (w_words[:, cols].bitcast(FP8X4), w_plane[:, cols])
@@ -96,74 +105,73 @@ def tile_picked_phglu_gelu_p_kernel(tc, x_words, x_scales, w1, w2, offs, out):
             nc.vector.tensor_copy(t[:], word_table[:].indirect(offsets[:, j0 // 16 : (j0 + width) // 16]))
             picked.append((t, j0, width))
 
-        banks = {}
-        for m in range(2):
-            for h in range(2):
-                for a in range(2):
-                    banks[m, h, a] = psum.tile([P, N_TILE], F32, name=f"bank{m}{h}{a}")
+        banks = [psum.tile([P, N_TILE], F32, name=f"bank{b}") for b in range(8)]
 
-        def warm_up():
-            w_words, w_plane = codes[0, 0]
-            for r in range(8):
+        def warm_up(passes):
+            for r in range(passes):
                 nc.tensor.matmul_mx(
-                    out=banks[1, 1, r // 4][:, (r % 4) * 128 : (r % 4 + 1) * 128],
-                    lhsT=w_words,
-                    lhsT_scale=w_plane,
-                    rhs=w_words,
-                    rhs_scale=w_plane,
+                    out=banks[6 + r // 2][:, (r % 2) * N : (r % 2 + 1) * N],
+                    lhsT=codes[0, 0][0],
+                    lhsT_scale=codes[0, 0][1],
+                    rhs=codes["w1"][0],
+                    rhs_scale=codes["w1"][1],
                     start=True,
                     stop=True,
                 )
 
-        def product(m, h, a):
-            w_words, w_plane = codes[m, a]
-            for t, j0, width in picked:
-                if j0 // N_TILE == h:
-                    nc.tensor.matmul_mx(
-                        out=banks[m, h, a][:, j0 % N_TILE : j0 % N_TILE + width],
-                        lhsT=w_words,
-                        lhsT_scale=w_plane,
-                        rhs=t[:].bitcast(FP8X4),
-                        rhs_scale=plane_of(j0, width),
-                        start=True,
-                        stop=True,
-                    )
+        sums = {}
 
-        def finish(m, h, widths, tag):
-            gate = keep.tile([P, N_TILE], F32, name=f"gate{m}{h}", tag=tag)
-            c0 = 0
-            for width in widths:
-                cols = slice(c0, c0 + width)
-                nc.scalar.activation(gate[:, cols], banks[m, h, 0][:, cols], GELU)
-                res = keep.tile([P, width], F32, name=f"res{m}{h}{c0}")
-                nc.vector.tensor_tensor(res[:], gate[:, cols], banks[m, h, 1][:, cols], MULT)
-                j0 = h * N_TILE + c0
-                nc.sync.dma_start(out[m * M_TILE : (m + 1) * M_TILE, j0 : j0 + width], res[:])
-                c0 = c0 + width
+        def product(m, a, piece, bank, c0=0):
+            w_words, w_plane = codes[m, a]
+            t, j0, width = picked[piece]
+            sums[m, a, piece] = banks[bank][:, c0 : c0 + width]
+            nc.tensor.matmul_mx(
+                out=sums[m, a, piece],
+                lhsT=w_words,
+                lhsT_scale=w_plane,
+                rhs=t[:].bitcast(FP8X4),
+                rhs_scale=plane_of(j0, width),
+                start=True,
+                stop=True,
+            )
+
+        def finish(m, j0, width, gate_sums, value_sums):
+            gate = keep.tile([P, width], F32, name=f"gate{m}{j0}")
+            nc.scalar.activation(gate[:], gate_sums, GELU)
+            res = keep.tile([P, width], F32, name=f"res{m}{j0}")
+            nc.vector.tensor_tensor(res[:], gate[:], value_sums, MULT)
+            nc.sync.dma_start(out[m * M_TILE : (m + 1) * M_TILE, j0 : j0 + width], res[:])
 
         load_w(0, 0)
         load_scales()
-        load_words()
-        load_w(0, 1)
         load_w(1, 0)
+        load_words(2)
+        load_w(0, 1)
+        load_w(1, 1)
         warm_table()
-        scales(0, 1024)
-        quantize_w([(0, 0)], "q00")
-        load_w(1, 1, "q00")
-        warm_up()
-        gather(0, 512, "picked0")
-        gather(512, 512, "picked512")
-        quantize_w([(0, 1), (1, 0)], "q01", "word_table")
-        quantize_w([(1, 1)], "q11", None, nc.vector.tensor_copy)
-        product(0, 0, 0)
-        product(0, 1, 0)
-        product(0, 0, 1)
-        finish(0, 0, [512], "gate00")
-        product(1, 0, 0)
-        product(0, 1, 1)
-        finish(0, 1, [512], "gate01")
-        product(1, 1, 0)
-        product(1, 0, 1)
-        finish(1, 0, [512], "gate10")
-        product(1, 1, 1)
-        finish(1, 1, [256, 256], "gate11")
+        gather_scales(0, 512)
+        move_scales(0, 512, nc.sync)
+        gather_scales(512, 512)
+        move_scales(512, 512, nc.sync)
+        quantize_w([(0, 0), (1, 0)], "w1")
+        warm_up(3)
+        gather(0, 256, "picked0")
+        gather(256, 256, "picked256")
+        quantize_w([(0, 1)], "w2a")
+        gather(512, 256, "picked512")
+        quantize_w([(1, 1)], "w2b")
+        gather(768, 256, "raw11")
+        for piece in range(2):
+            for m in range(2):
+                product(m, 0, piece, m, piece * 256)
+        for m in range(2):
+            for piece in range(2):
+                product(m, 1, piece, 2 + m, piece * 256)
+        for m in range(2):
+            finish(m, 0, 512, banks[m][:], banks[2 + m][:])
+        for piece in (2, 3):
+            for a in range(2):
+                for m in range(2):
+                    product(m, a, piece, 2 * piece + a, m * 256)
+            for m in range(2):
+                finish(m, piece * 256, 256, sums[m, 0, piece], sums[m, 1, piece])

@@ -49,6 +49,13 @@ def tile_picked_phglu_gelu_p_kernel(tc, x_words, x_scales, w1, w2, offs, out):
             nc.sync.dma_start(t[:], weights[a][:, m * M_TILE : (m + 1) * M_TILE].rearrange("(p j) c -> p j c", j=PACK))
             raw[m, a] = t[:]
 
+        w1_rows = keep.tile([P, PACK, N], F32, name="w1_rows", align_bytes=64)
+        for m in range(2):
+            raw[m, 0] = w1_rows[:, :, m * M_TILE : (m + 1) * M_TILE]
+
+        def load_w1(j0):
+            nc.sync.dma_start(w1_rows[:, j0 : j0 + 2], w1.rearrange("(p j) c -> p j c", j=PACK)[:, j0 : j0 + 2])
+
         planes = []
         picked_scales = {}
 
@@ -142,9 +149,9 @@ def tile_picked_phglu_gelu_p_kernel(tc, x_words, x_scales, w1, w2, offs, out):
             nc.vector.tensor_tensor(res[:], gate[:], value_sums, MULT)
             nc.sync.dma_start(out[m * M_TILE : (m + 1) * M_TILE, j0 : j0 + width], res[:])
 
-        load_w(0, 0)
+        load_w1(0)
         load_scales()
-        load_w(1, 0)
+        load_w1(2)
         load_words(2)
         load_w(0, 1)
         load_w(1, 1)
@@ -161,12 +168,10 @@ def tile_picked_phglu_gelu_p_kernel(tc, x_words, x_scales, w1, w2, offs, out):
         gather(512, 256, "picked512")
         quantize_w([(1, 1)], "w2b")
         gather(768, 256, "raw11")
-        for piece in range(2):
-            for m in range(2):
-                product(m, 0, piece, m, piece * 256)
         for m in range(2):
-            for piece in range(2):
-                product(m, 1, piece, 2 + m, piece * 256)
+            for a in range(2):
+                for piece in range(2):
+                    product(m, a, piece, 2 * a + m, piece * 256)
         for m in range(2):
             finish(m, 0, 512, banks[m][:], banks[2 + m][:])
         for piece in (2, 3):

@@ -26,157 +26,144 @@ def tile_picked_phglu_gelu_p_kernel(tc, x_words, x_scales, w1, w2, offs, out):
     with ExitStack() as ctx:
         keep = ctx.enter_context(tc.tile_pool(name="keep", bufs=1))
         psum = ctx.enter_context(tc.psum_pool(name="psum", bufs=1))
-        weights = (w1, w2)
 
         offsets = keep.tile([P, S // 16], U16, name="offsets")
         nc.sync.dma_start(offsets[:], offs)
 
         scale_table = keep.tile([P, T], U8, name="scale_table", align_bytes=64)
         nc.vector.memset(scale_table[:].bitcast(I32), 0)
+        plane_spans = ((0, 768), (768, 256))
+        planes = [keep.tile([P, width], U8, name=f"x_plane{j0}", align_bytes=64) for j0, width in plane_spans]
+        for plane in planes:
+            nc.vector.memset(plane[:].bitcast(I32), 0)
         word_table = keep.tile([P, T], U32, name="word_table", tag="word_table", align_bytes=64)
         raw = {}
 
-        def load_scales():
-            nc.sync.dma_start(scale_table[0:P:8, :].bitcast(I32), x_scales[0].bitcast(I32))
-
-        def load_words(parts):
-            source = x_words[0].rearrange("p c r -> p (c r)").bitcast(I32)
-            for c0 in range(0, T, T // parts):
-                nc.sync.dma_start(word_table[:, c0 : c0 + T // parts].bitcast(I32), source[:, c0 : c0 + T // parts])
-
-        def load_w(m, a, tag=None):
-            t = keep.tile([P, PACK, M_TILE], F32, name=f"raw{m}{a}", tag=tag or f"raw{m}{a}", align_bytes=64)
-            nc.sync.dma_start(t[:], weights[a][:, m * M_TILE : (m + 1) * M_TILE].rearrange("(p j) c -> p j c", j=PACK))
+        def load_w(m, a):
+            t = keep.tile([P, PACK, M_TILE], F32, name=f"raw{m}{a}", tag=f"raw{m}{a}", align_bytes=64)
+            nc.sync.dma_start(t[:], (w1, w2)[a][:, m * M_TILE : (m + 1) * M_TILE].rearrange("(p j) c -> p j c", j=PACK))
             raw[m, a] = t[:]
 
-        w1_rows = keep.tile([P, PACK, N], F32, name="w1_rows", align_bytes=64)
-        for m in range(2):
-            raw[m, 0] = w1_rows[:, :, m * M_TILE : (m + 1) * M_TILE]
+        words = x_words[0].rearrange("p c r -> p (c r)").bitcast(I32)
+        load_w(0, 0)
+        nc.sync.dma_start(scale_table[0:P:8, :].bitcast(I32), x_scales[0].bitcast(I32))
+        for c0 in range(0, T, T // 2):
+            nc.sync.dma_start(word_table[:, c0 : c0 + T // 2].bitcast(I32), words[:, c0 : c0 + T // 2])
+        load_w(0, 1)
+        load_w(1, 0)
+        load_w(1, 1)
 
-        def load_w1(j0):
-            nc.sync.dma_start(w1_rows[:, j0 : j0 + 2], w1.rearrange("(p j) c -> p j c", j=PACK)[:, j0 : j0 + 2])
+        warm = keep.tile([P, 2], F32, name="warm")
+        nc.gpsimd.memset(warm[:, 0:1], 0.0)
+        nc.scalar.activation(warm[:, 1:2], warm[:, 0:1], GELU)
 
-        planes = []
-        picked_scales = {}
-
-        def gather_scales(j0, width):
-            h0 = j0 // N_TILE * N_TILE
-            if j0 == h0:
-                picked_scales[h0] = keep.tile([P, N_TILE], U8, name=f"picked_scales{h0}", align_bytes=64)
-            nc.vector.tensor_copy(
-                picked_scales[h0][:, j0 - h0 : j0 - h0 + width],
-                scale_table[:].indirect(offsets[:, j0 // 16 : (j0 + width) // 16]),
-            )
-
-        def move_scales(j0, width, queue):
-            plane = keep.tile([P, width], U8, name=f"x_plane{j0}", align_bytes=64)
-            nc.vector.memset(plane[:].bitcast(I32), 0)
+        for plane, (j0, width) in zip(planes, plane_spans):
+            picked_scales = keep.tile([P, width], U8, name=f"picked_scales{j0}", align_bytes=64)
+            nc.vector.tensor_copy(picked_scales[:], scale_table[:].indirect(offsets[:, j0 // 16 : (j0 + width) // 16]))
             for i in range(4):
-                queue.dma_start(plane[i:P:32, :].bitcast(I32), picked_scales[j0][8 * i : P : 32, :].bitcast(I32))
-            planes.append((plane, j0, width))
-
-        def plane_of(j0, width):
-            for plane, p0, pw in planes:
-                if p0 <= j0 and j0 + width <= p0 + pw:
-                    return plane[:, j0 - p0 : j0 - p0 + width]
-
-        def warm_table():
-            warm = keep.tile([P, 2], F32, name="warm")
-            nc.gpsimd.memset(warm[:, 0:1], 0.0)
-            nc.scalar.activation(warm[:, 1:2], warm[:, 0:1], GELU)
+                nc.sync.dma_start(plane[i:P:32, :].bitcast(I32), picked_scales[8 * i : P : 32, :].bitcast(I32))
 
         codes = {}
 
-        def cast_w(piece, target):
-            nc.scalar.copy(target.rearrange("p (c i) j -> p c j i", i=4), raw[piece].rearrange("p j (c i) -> p c j i", i=4))
-
-        def quantize_w(pieces, name):
-            n = len(pieces)
-            grouped = keep.tile([P, n * M_TILE, PACK], BF16, name=f"grouped{name}", align_bytes=64)
-            for i, piece in enumerate(pieces):
-                cast_w(piece, grouped[:, i * M_TILE : (i + 1) * M_TILE])
-            w_words = keep.tile([P, n * M_TILE], U32, name=f"w_words{name}", align_bytes=64)
-            w_plane = keep.tile([P, n * M_TILE], U8, name=f"w_plane{name}", align_bytes=64)
+        def quantize_w(m, a, words_tag=None, cast=nc.scalar.copy):
+            grouped = keep.tile([P, M_TILE, PACK], BF16, name=f"grouped{m}{a}", tag=f"grouped{m}{a}", align_bytes=64)
+            cast(grouped[:].rearrange("p (c i) j -> p c j i", i=4), raw[m, a].rearrange("p j (c i) -> p c j i", i=4))
+            w_words = keep.tile([P, M_TILE], U32, name=f"w_words{m}{a}", tag=words_tag or f"w_words{m}{a}", align_bytes=64)
+            w_plane = keep.tile([P, M_TILE], U8, name=f"w_plane{m}{a}", align_bytes=64)
             nc.vector.quantize_mx(
                 out=w_words[:].bitcast(FP8X4), scales=w_plane[:], in_=grouped[:].rearrange("p c j -> p (c j)")
             )
-            codes[name] = (w_words[:].bitcast(FP8X4), w_plane[:])
-            for i, piece in enumerate(pieces):
-                cols = slice(i * M_TILE, (i + 1) * M_TILE)
-                codes[piece] = (w_words[:, cols].bitcast(FP8X4), w_plane[:, cols])
+            codes[m, a] = (w_words[:].bitcast(FP8X4), w_plane[:])
 
-        picked = []
+        banks = [[psum.tile([P, N_TILE], F32, name=f"bank{b}{a}") for a in range(2)] for b in range(4)]
 
-        def gather(j0, width, tag):
-            t = keep.tile([P, width], U32, name=f"picked{j0}", tag=tag, align_bytes=64)
-            nc.vector.tensor_copy(t[:], word_table[:].indirect(offsets[:, j0 // 16 : (j0 + width) // 16]))
-            picked.append((t, j0, width))
-
-        banks = [psum.tile([P, N_TILE], F32, name=f"bank{b}") for b in range(8)]
-
-        def warm_up(passes):
-            for r in range(passes):
-                nc.tensor.matmul_mx(
-                    out=banks[6 + r // 2][:, (r % 2) * N : (r % 2 + 1) * N],
-                    lhsT=codes[0, 0][0],
-                    lhsT_scale=codes[0, 0][1],
-                    rhs=codes["w1"][0],
-                    rhs_scale=codes["w1"][1],
-                    start=True,
-                    stop=True,
-                )
-
-        sums = {}
-
-        def product(m, a, piece, bank, c0=0):
-            w_words, w_plane = codes[m, a]
-            t, j0, width = picked[piece]
-            sums[m, a, piece] = banks[bank][:, c0 : c0 + width]
+        quantize_w(0, 0)
+        for r in range(8):
             nc.tensor.matmul_mx(
-                out=sums[m, a, piece],
-                lhsT=w_words,
-                lhsT_scale=w_plane,
-                rhs=t[:].bitcast(FP8X4),
-                rhs_scale=plane_of(j0, width),
+                out=banks[3][r // 4][:, (r % 4) * M_TILE : (r % 4 + 1) * M_TILE],
+                lhsT=codes[0, 0][0],
+                lhsT_scale=codes[0, 0][1],
+                rhs=codes[0, 0][0],
+                rhs_scale=codes[0, 0][1],
                 start=True,
                 stop=True,
             )
 
-        def finish(m, j0, width, gate_sums, value_sums):
-            gate = keep.tile([P, width], F32, name=f"gate{m}{j0}")
-            nc.scalar.activation(gate[:], gate_sums, GELU)
-            res = keep.tile([P, width], F32, name=f"res{m}{j0}")
-            nc.vector.tensor_tensor(res[:], gate[:], value_sums, MULT)
-            nc.sync.dma_start(out[m * M_TILE : (m + 1) * M_TILE, j0 : j0 + width], res[:])
+        picked = {}
 
-        load_w1(0)
-        load_scales()
-        load_w1(2)
-        load_words(2)
-        load_w(0, 1)
-        load_w(1, 1)
-        warm_table()
-        gather_scales(0, 512)
-        move_scales(0, 512, nc.sync)
-        gather_scales(512, 512)
-        move_scales(512, 512, nc.sync)
-        quantize_w([(0, 0), (1, 0)], "w1")
-        warm_up(3)
-        gather(0, 256, "picked0")
-        gather(256, 256, "picked256")
-        quantize_w([(0, 1)], "w2a")
+        def gather(j0, width, tag):
+            t = keep.tile([P, width], U32, name=f"picked{j0}", tag=tag, align_bytes=64)
+            nc.vector.tensor_copy(t[:], word_table[:].indirect(offsets[:, j0 // 16 : (j0 + width) // 16]))
+            picked[j0] = t
+
+        gather(0, 512, "picked0")
         gather(512, 256, "picked512")
-        quantize_w([(1, 1)], "w2b")
-        gather(768, 256, "raw11")
-        for m in range(2):
-            for a in range(2):
-                for piece in range(2):
-                    product(m, a, piece, 2 * a + m, piece * 256)
-        for m in range(2):
-            finish(m, 0, 512, banks[m][:], banks[2 + m][:])
-        for piece in (2, 3):
-            for a in range(2):
-                for m in range(2):
-                    product(m, a, piece, 2 * piece + a, m * 256)
-            for m in range(2):
-                finish(m, piece * 256, 256, sums[m, 0, piece], sums[m, 1, piece])
+        quantize_w(0, 1)
+        quantize_w(1, 0)
+        gather(768, 256, "raw10")
+        quantize_w(1, 1)
+
+        blocks = (
+            ((0, 0, 512),),
+            ((0, 512, 256), (1, 512, 256)),
+            ((1, 0, 512),),
+            ((0, 768, 256), (1, 768, 256)),
+        )
+
+        sums = {}
+
+        def multiply(target, m, a, source, j0, width):
+            p = 0 if j0 < plane_spans[1][0] else 1
+            p0 = j0 - plane_spans[p][0]
+            nc.tensor.matmul_mx(
+                out=target,
+                lhsT=codes[m, a][0],
+                lhsT_scale=codes[m, a][1],
+                rhs=picked[source][:, j0 - source : j0 - source + width].bitcast(FP8X4),
+                rhs_scale=planes[p][:, p0 : p0 + width],
+                start=True,
+                stop=True,
+            )
+
+        def product(b, a):
+            c0 = 0
+            for m, j0, width in blocks[b]:
+                multiply(banks[b][a][:, c0 : c0 + width], m, a, j0, j0, width)
+                c0 = c0 + width
+            for u in range(2):
+                sums[b, a, u] = banks[b][a][:, u * 256 : (u + 1) * 256]
+
+        def first_gate():
+            for u in range(2):
+                sums[0, 0, u] = banks[3 * u][0][:, 0:256]
+                multiply(sums[0, 0, u], 0, 0, 0, u * 256, 256)
+
+        def finish(b, stores):
+            gate = keep.tile([P, N_TILE], F32, name=f"gate{b}")
+            res = keep.tile([P, N_TILE], F32, name=f"res{b}")
+            m, j0, width = blocks[b][0]
+            if width == N_TILE:
+                target = out[m * M_TILE : (m + 1) * M_TILE, j0 : j0 + width].rearrange("p (u c) -> p u c", u=2)
+            else:
+                target = out[:, j0 : j0 + width].rearrange("(u p) c -> p u c", u=2)
+            for u in range(2):
+                cols = slice(u * 256, (u + 1) * 256)
+                nc.scalar.activation(gate[:, cols], sums[b, 0, u], GELU)
+                nc.vector.tensor_tensor(res[:, cols], gate[:, cols], sums[b, 1, u], MULT)
+                if stores == 2:
+                    nc.sync.dma_start(target[:, u], res[:, cols])
+            if stores == 1:
+                nc.sync.dma_start(target, res[:].rearrange("p (u c) -> p u c", u=2))
+
+        first_gate()
+        product(0, 1)
+        finish(0, 2)
+        product(1, 0)
+        product(1, 1)
+        finish(1, 1)
+        product(2, 0)
+        product(2, 1)
+        finish(2, 1)
+        product(3, 0)
+        product(3, 1)
+        finish(3, 2)

@@ -14,6 +14,7 @@ U8 = mybir.dt.uint8
 FP8X4 = mybir.dt.float8_e4m3fn_x4
 GELU = mybir.ActivationFunctionType.Gelu_apprx_tanh
 MULT = mybir.AluOpType.mult
+ADD = mybir.AluOpType.add
 
 P = 128
 PACK = 4
@@ -49,9 +50,12 @@ def tile_picked_phglu_gelu_p_kernel(tc, x_words, x_scales, w1, w2, offs, out):
         nc.sync.dma_start(scale_table[0:P:8, :].bitcast(I32), x_scales[0].bitcast(I32))
         for c0 in range(0, T, T // 2):
             nc.sync.dma_start(word_table[:, c0 : c0 + T // 2].bitcast(I32), words[:, c0 : c0 + T // 2])
-        load_w(0, 1)
+        w2_rows = keep.tile([P, PACK, N], F32, name="w2_rows", align_bytes=64)
+        for j0 in (0, 2):
+            nc.sync.dma_start(w2_rows[:, j0 : j0 + 2], w2.rearrange("(p j) c -> p j c", j=PACK)[:, j0 : j0 + 2])
+        for m in range(2):
+            raw[m, 1] = w2_rows[:, :, m * M_TILE : (m + 1) * M_TILE]
         load_w(1, 0)
-        load_w(1, 1)
 
         warm = keep.tile([P, 2], F32, name="warm")
         nc.gpsimd.memset(warm[:, 0:1], 0.0)
@@ -67,7 +71,12 @@ def tile_picked_phglu_gelu_p_kernel(tc, x_words, x_scales, w1, w2, offs, out):
 
         def quantize_w(m, a, words_tag=None, cast=nc.scalar.copy):
             grouped = keep.tile([P, M_TILE, PACK], BF16, name=f"grouped{m}{a}", tag=f"grouped{m}{a}", align_bytes=64)
-            cast(grouped[:].rearrange("p (c i) j -> p c j i", i=4), raw[m, a].rearrange("p j (c i) -> p c j i", i=4))
+            if (m, a) == (1, 1):
+                nc.gpsimd.tensor_scalar(
+                    out=grouped[:], in0=raw[m, a].rearrange("p j c -> p c j"), scalar1=1.0, scalar2=0.0, op0=MULT, op1=ADD
+                )
+            else:
+                cast(grouped[:].rearrange("p (c i) j -> p c j i", i=4), raw[m, a].rearrange("p j (c i) -> p c j i", i=4))
             w_words = keep.tile([P, M_TILE], U32, name=f"w_words{m}{a}", tag=words_tag or f"w_words{m}{a}", align_bytes=64)
             w_plane = keep.tile([P, M_TILE], U8, name=f"w_plane{m}{a}", align_bytes=64)
             nc.vector.quantize_mx(
@@ -99,9 +108,9 @@ def tile_picked_phglu_gelu_p_kernel(tc, x_words, x_scales, w1, w2, offs, out):
         gather(0, 512, "picked0")
         gather(512, 256, "picked512")
         quantize_w(0, 1)
+        quantize_w(1, 1)
         quantize_w(1, 0)
         gather(768, 256, "raw10")
-        quantize_w(1, 1)
 
         blocks = (
             ((0, 0, 512),),

@@ -147,7 +147,7 @@ def tile_picked_phglu_gelu_p_kernel(tc, x_words, x_scales, w1, w2, offs, out):
                 sums[0, 0, u] = banks[3 * u][0][:, 0:256]
                 multiply(sums[0, 0, u], 0, 0, 0, u * 256, 256)
 
-        def finish(b, stores):
+        def finish(b, stores, pieces=((0, 0, 256), (1, 0, 256))):
             gate = keep.tile([P, N_TILE], F32, name=f"gate{b}")
             res = keep.tile([P, N_TILE], F32, name=f"res{b}")
             m, j0, width = blocks[b][0]
@@ -155,12 +155,12 @@ def tile_picked_phglu_gelu_p_kernel(tc, x_words, x_scales, w1, w2, offs, out):
                 target = out[m * M_TILE : (m + 1) * M_TILE, j0 : j0 + width].rearrange("p (u c) -> p u c", u=2)
             else:
                 target = out[:, j0 : j0 + width].rearrange("(u p) c -> p u c", u=2)
-            for u in range(2):
-                cols = slice(u * 256, (u + 1) * 256)
-                nc.scalar.activation(gate[:, cols], sums[b, 0, u], GELU)
-                nc.vector.tensor_tensor(res[:, cols], gate[:, cols], sums[b, 1, u], MULT)
+            for u, c0, n in pieces:
+                cols = slice(u * 256 + c0, u * 256 + c0 + n)
+                nc.scalar.activation(gate[:, cols], sums[b, 0, u][:, c0 : c0 + n], GELU)
+                nc.vector.tensor_tensor(res[:, cols], gate[:, cols], sums[b, 1, u][:, c0 : c0 + n], MULT)
                 if stores == 2:
-                    nc.sync.dma_start(target[:, u], res[:, cols])
+                    nc.sync.dma_start(target[:, u, c0 : c0 + n], res[:, cols])
             if stores == 1:
                 nc.sync.dma_start(target, res[:].rearrange("p (u c) -> p u c", u=2))
 
@@ -175,4 +175,4 @@ def tile_picked_phglu_gelu_p_kernel(tc, x_words, x_scales, w1, w2, offs, out):
         finish(2, 1)
         product(3, 0)
         product(3, 1)
-        finish(3, 2)
+        finish(3, 2, ((0, 0, 256), (1, 0, 128), (1, 128, 128)))

@@ -37,6 +37,10 @@ def tile_picked_phglu_gelu_p_kernel(tc, x_words, x_scales, w1, w2, offs, out):
         planes = [keep.tile([P, width], U8, name=f"x_plane{j0}", align_bytes=64) for j0, width in plane_spans]
         for plane in planes:
             nc.vector.memset(plane[:].bitcast(I32), 0)
+        w_words = keep.tile([P, 4 * M_TILE], U32, name="w_words", align_bytes=64)
+        w_plane = keep.tile([P, 4 * M_TILE], U8, name="w_plane", align_bytes=64)
+        nc.vector.memset(w_words[:].bitcast(I32), 0)
+        nc.vector.memset(w_plane[:].bitcast(I32), 0)
         word_table = keep.tile([P, T], U32, name="word_table", tag="word_table", align_bytes=64)
         raw = {}
 
@@ -69,7 +73,7 @@ def tile_picked_phglu_gelu_p_kernel(tc, x_words, x_scales, w1, w2, offs, out):
 
         codes = {}
 
-        def quantize_w(m, a, words_tag=None, cast=nc.scalar.copy):
+        def quantize_w(m, a, cast=nc.scalar.copy):
             grouped = keep.tile([P, M_TILE, PACK], BF16, name=f"grouped{m}{a}", tag=f"grouped{m}{a}", align_bytes=64)
             if (m, a) == (1, 1):
                 nc.gpsimd.tensor_scalar(
@@ -77,23 +81,22 @@ def tile_picked_phglu_gelu_p_kernel(tc, x_words, x_scales, w1, w2, offs, out):
                 )
             else:
                 cast(grouped[:].rearrange("p (c i) j -> p c j i", i=4), raw[m, a].rearrange("p j (c i) -> p c j i", i=4))
-            w_words = keep.tile([P, M_TILE], U32, name=f"w_words{m}{a}", tag=words_tag or f"w_words{m}{a}", align_bytes=64)
-            w_plane = keep.tile([P, M_TILE], U8, name=f"w_plane{m}{a}", align_bytes=64)
+            cols = slice((2 * a + m) * M_TILE, (2 * a + m + 1) * M_TILE)
             nc.vector.quantize_mx(
-                out=w_words[:].bitcast(FP8X4), scales=w_plane[:], in_=grouped[:].rearrange("p c j -> p (c j)")
+                out=w_words[:, cols].bitcast(FP8X4), scales=w_plane[:, cols], in_=grouped[:].rearrange("p c j -> p (c j)")
             )
-            codes[m, a] = (w_words[:].bitcast(FP8X4), w_plane[:])
+            codes[m, a] = (w_words[:, cols].bitcast(FP8X4), w_plane[:, cols])
 
         banks = [[psum.tile([P, N_TILE], F32, name=f"bank{b}{a}") for a in range(2)] for b in range(4)]
 
         quantize_w(0, 0)
-        for r in range(8):
+        for bank in banks[3]:
             nc.tensor.matmul_mx(
-                out=banks[3][r // 4][:, (r % 4) * M_TILE : (r % 4 + 1) * M_TILE],
+                out=bank[:],
                 lhsT=codes[0, 0][0],
                 lhsT_scale=codes[0, 0][1],
-                rhs=codes[0, 0][0],
-                rhs_scale=codes[0, 0][1],
+                rhs=w_words[:].bitcast(FP8X4),
+                rhs_scale=w_plane[:],
                 start=True,
                 stop=True,
             )
@@ -136,9 +139,11 @@ def tile_picked_phglu_gelu_p_kernel(tc, x_words, x_scales, w1, w2, offs, out):
 
         def product(b, a):
             c0 = 0
+            step = 128 if b == 3 else 256
             for m, j0, width in blocks[b]:
-                multiply(banks[b][a][:, c0 : c0 + width], m, a, j0, j0, width)
-                c0 = c0 + width
+                for j in range(j0, j0 + width, step):
+                    multiply(banks[b][a][:, c0 : c0 + step], m, a, j0, j, step)
+                    c0 = c0 + step
             for u in range(2):
                 sums[b, a, u] = banks[b][a][:, u * 256 : (u + 1) * 256]
 

@@ -55,8 +55,7 @@ def tile_picked_phglu_gelu_p_kernel(tc, x_words, x_scales, w1, w2, offs, out):
         for c0 in range(0, T, T // 2):
             nc.sync.dma_start(word_table[:, c0 : c0 + T // 2].bitcast(I32), words[:, c0 : c0 + T // 2])
         w2_rows = keep.tile([P, PACK, N], F32, name="w2_rows", align_bytes=64)
-        for j0 in (0, 2):
-            nc.sync.dma_start(w2_rows[:, j0 : j0 + 2], w2.rearrange("(p j) c -> p j c", j=PACK)[:, j0 : j0 + 2])
+        nc.sync.dma_start(w2_rows[:], w2.rearrange("(p j) c -> p j c", j=PACK))
         for m in range(2):
             raw[m, 1] = w2_rows[:, :, m * M_TILE : (m + 1) * M_TILE]
         load_w(1, 0)
@@ -69,28 +68,31 @@ def tile_picked_phglu_gelu_p_kernel(tc, x_words, x_scales, w1, w2, offs, out):
             picked_scales = keep.tile([P, width], U8, name=f"picked_scales{j0}", align_bytes=64)
             nc.vector.tensor_copy(picked_scales[:], scale_table[:].indirect(offsets[:, j0 // 16 : (j0 + width) // 16]))
             for i in range(4):
-                nc.sync.dma_start(plane[i:P:32, :].bitcast(I32), picked_scales[8 * i : P : 32, :].bitcast(I32))
+                queue = nc.scalar if j0 == 0 and i % 2 else nc.sync
+                queue.dma_start(plane[i:P:32, :].bitcast(I32), picked_scales[8 * i : P : 32, :].bitcast(I32))
 
         codes = {}
 
-        def quantize_w(m, a, cast=nc.scalar.copy):
+        def quantize_w(m, a):
             grouped = keep.tile([P, M_TILE, PACK], BF16, name=f"grouped{m}{a}", tag=f"grouped{m}{a}", align_bytes=64)
             if (m, a) == (1, 1):
                 nc.gpsimd.tensor_scalar(
                     out=grouped[:], in0=raw[m, a].rearrange("p j c -> p c j"), scalar1=1.0, scalar2=0.0, op0=MULT, op1=ADD
                 )
             else:
-                cast(grouped[:].rearrange("p (c i) j -> p c j i", i=4), raw[m, a].rearrange("p j (c i) -> p c j i", i=4))
+                nc.scalar.copy(
+                    grouped[:].rearrange("p (c i) j -> p c j i", i=4), raw[m, a].rearrange("p j (c i) -> p c j i", i=4)
+                )
             cols = slice((2 * a + m) * M_TILE, (2 * a + m + 1) * M_TILE)
             nc.vector.quantize_mx(
                 out=w_words[:, cols].bitcast(FP8X4), scales=w_plane[:, cols], in_=grouped[:].rearrange("p c j -> p (c j)")
             )
             codes[m, a] = (w_words[:, cols].bitcast(FP8X4), w_plane[:, cols])
 
-        banks = [[psum.tile([P, N_TILE], F32, name=f"bank{b}{a}") for a in range(2)] for b in range(4)]
+        banks = [psum.tile([P, N_TILE], F32, name=f"bank{b}") for b in range(8)]
 
         quantize_w(0, 0)
-        for bank in banks[3]:
+        for bank in banks[6:]:
             nc.tensor.matmul_mx(
                 out=bank[:],
                 lhsT=codes[0, 0][0],
@@ -106,7 +108,8 @@ def tile_picked_phglu_gelu_p_kernel(tc, x_words, x_scales, w1, w2, offs, out):
         def gather(j0, width, tag):
             t = keep.tile([P, width], U32, name=f"picked{j0}", tag=tag, align_bytes=64)
             nc.vector.tensor_copy(t[:], word_table[:].indirect(offsets[:, j0 // 16 : (j0 + width) // 16]))
-            picked[j0] = t
+            for c0 in range(0, width, 256):
+                picked[(j0 + c0) // 256] = t[:, c0 : c0 + 256]
 
         gather(0, 512, "picked0")
         gather(512, 256, "picked512")
@@ -115,69 +118,67 @@ def tile_picked_phglu_gelu_p_kernel(tc, x_words, x_scales, w1, w2, offs, out):
         quantize_w(1, 0)
         gather(768, 256, "raw10")
 
-        blocks = (
-            ((0, 0, 512),),
-            ((0, 512, 256), (1, 512, 256)),
-            ((1, 0, 512),),
-            ((0, 768, 256), (1, 768, 256)),
-        )
-
         sums = {}
+        gates = {}
 
-        def multiply(target, m, a, source, j0, width):
-            p = 0 if j0 < plane_spans[1][0] else 1
-            p0 = j0 - plane_spans[p][0]
-            nc.tensor.matmul_mx(
-                out=target,
-                lhsT=codes[m, a][0],
-                lhsT_scale=codes[m, a][1],
-                rhs=picked[source][:, j0 - source : j0 - source + width].bitcast(FP8X4),
-                rhs_scale=planes[p][:, p0 : p0 + width],
-                start=True,
-                stop=True,
-            )
+        def multiply(m, q, a, bank, half):
+            sums[m, q, a] = banks[bank][:, half * 256 : (half + 1) * 256]
+            scales = planes[0][:, q * 256 : (q + 1) * 256] if q < 3 else planes[1][:]
+            width = 256 if q < 3 else 128
+            for c0 in range(0, 256, width):
+                cols = slice(c0, c0 + width)
+                nc.tensor.matmul_mx(
+                    out=sums[m, q, a][:, cols],
+                    lhsT=codes[m, a][0],
+                    lhsT_scale=codes[m, a][1],
+                    rhs=picked[q][:, cols].bitcast(FP8X4),
+                    rhs_scale=scales[:, cols],
+                    start=True,
+                    stop=True,
+                )
 
-        def product(b, a):
+        def gelu(m, q, pieces=(256,)):
+            gates[m, q] = keep.tile([P, 256], F32, name=f"gate{m}{q}")
             c0 = 0
-            step = 128 if b == 3 else 256
-            for m, j0, width in blocks[b]:
-                for j in range(j0, j0 + width, step):
-                    multiply(banks[b][a][:, c0 : c0 + step], m, a, j0, j, step)
-                    c0 = c0 + step
-            for u in range(2):
-                sums[b, a, u] = banks[b][a][:, u * 256 : (u + 1) * 256]
+            for n in pieces:
+                nc.scalar.activation(gates[m, q][:, c0 : c0 + n], sums[m, q, 0][:, c0 : c0 + n], GELU)
+                c0 = c0 + n
 
-        def first_gate():
-            for u in range(2):
-                sums[0, 0, u] = banks[3 * u][0][:, 0:256]
-                multiply(sums[0, 0, u], 0, 0, 0, u * 256, 256)
+        def finish(m, q, pieces=(256,)):
+            res = keep.tile([P, 256], F32, name=f"res{m}{q}")
+            c0 = 0
+            for n in pieces:
+                cols = slice(c0, c0 + n)
+                nc.vector.tensor_tensor(res[:, cols], gates[m, q][:, cols], sums[m, q, 1][:, cols], MULT)
+                nc.sync.dma_start(out[m * M_TILE : (m + 1) * M_TILE, q * 256 + c0 : q * 256 + c0 + n], res[:, cols])
+                c0 = c0 + n
 
-        def finish(b, stores, pieces=((0, 0, 256), (1, 0, 256))):
-            gate = keep.tile([P, N_TILE], F32, name=f"gate{b}")
-            res = keep.tile([P, N_TILE], F32, name=f"res{b}")
-            m, j0, width = blocks[b][0]
-            if width == N_TILE:
-                target = out[m * M_TILE : (m + 1) * M_TILE, j0 : j0 + width].rearrange("p (u c) -> p u c", u=2)
-            else:
-                target = out[:, j0 : j0 + width].rearrange("(u p) c -> p u c", u=2)
-            for u, c0, n in pieces:
-                cols = slice(u * 256 + c0, u * 256 + c0 + n)
-                nc.scalar.activation(gate[:, cols], sums[b, 0, u][:, c0 : c0 + n], GELU)
-                nc.vector.tensor_tensor(res[:, cols], gate[:, cols], sums[b, 1, u][:, c0 : c0 + n], MULT)
-                if stores == 2:
-                    nc.sync.dma_start(target[:, u, c0 : c0 + n], res[:, cols])
-            if stores == 1:
-                nc.sync.dma_start(target, res[:].rearrange("p (u c) -> p u c", u=2))
-
-        first_gate()
-        product(0, 1)
+        multiply(0, 0, 0, 0, 0)
+        multiply(0, 1, 0, 6, 0)
+        multiply(0, 0, 1, 1, 0)
+        multiply(0, 1, 1, 7, 0)
+        multiply(0, 2, 0, 2, 0)
+        multiply(1, 0, 0, 3, 0)
+        multiply(1, 1, 0, 3, 1)
+        multiply(0, 2, 1, 4, 0)
+        multiply(1, 2, 0, 5, 0)
+        for q in range(3):
+            gelu(0, q)
+        finish(0, 0)
+        finish(0, 1)
+        multiply(1, 0, 1, 0, 0)
+        multiply(1, 1, 1, 0, 1)
+        multiply(1, 2, 1, 1, 0)
+        multiply(0, 3, 0, 6, 0)
+        multiply(1, 3, 0, 2, 0)
+        multiply(0, 3, 1, 7, 0)
+        multiply(1, 3, 1, 7, 1)
+        for q in range(3):
+            gelu(1, q)
+        gelu(0, 3)
+        gelu(1, 3, (128, 128))
         finish(0, 2)
-        product(1, 0)
-        product(1, 1)
-        finish(1, 1)
-        product(2, 0)
-        product(2, 1)
-        finish(2, 1)
-        product(3, 0)
-        product(3, 1)
-        finish(3, 2, ((0, 0, 256), (1, 0, 128), (1, 128, 128)))
+        for q in range(3):
+            finish(1, q)
+        finish(0, 3)
+        finish(1, 3, (128, 128))

@@ -118,67 +118,73 @@ def tile_picked_phglu_gelu_p_kernel(tc, x_words, x_scales, w1, w2, offs, out):
         quantize_w(1, 0)
         gather(768, 256, "raw10")
 
+        pieces = (
+            (0, 0, 128),
+            (0, 128, 128),
+            (0, 256, 256),
+            (0, 512, 256),
+            (1, 0, 256),
+            (1, 256, 256),
+            (1, 512, 256),
+            (0, 768, 256),
+            (1, 768, 128),
+            (1, 896, 128),
+        )
         sums = {}
         gates = {}
 
-        def multiply(m, q, a, bank, half):
-            sums[m, q, a] = banks[bank][:, half * 256 : (half + 1) * 256]
-            scales = planes[0][:, q * 256 : (q + 1) * 256] if q < 3 else planes[1][:]
-            width = 256 if q < 3 else 128
-            for c0 in range(0, 256, width):
-                cols = slice(c0, c0 + width)
-                nc.tensor.matmul_mx(
-                    out=sums[m, q, a][:, cols],
-                    lhsT=codes[m, a][0],
-                    lhsT_scale=codes[m, a][1],
-                    rhs=picked[q][:, cols].bitcast(FP8X4),
-                    rhs_scale=scales[:, cols],
-                    start=True,
-                    stop=True,
-                )
+        def multiply(i, a, bank, c0):
+            m, j0, width = pieces[i]
+            h = 0 if j0 < plane_spans[1][0] else 1
+            p0 = j0 - plane_spans[h][0]
+            sums[i, a] = banks[bank][:, c0 : c0 + width]
+            nc.tensor.matmul_mx(
+                out=sums[i, a],
+                lhsT=codes[m, a][0],
+                lhsT_scale=codes[m, a][1],
+                rhs=picked[j0 // 256][:, j0 % 256 : j0 % 256 + width].bitcast(FP8X4),
+                rhs_scale=planes[h][:, p0 : p0 + width],
+                start=True,
+                stop=True,
+            )
 
-        def gelu(m, q, pieces=(256,)):
-            gates[m, q] = keep.tile([P, 256], F32, name=f"gate{m}{q}")
-            c0 = 0
-            for n in pieces:
-                nc.scalar.activation(gates[m, q][:, c0 : c0 + n], sums[m, q, 0][:, c0 : c0 + n], GELU)
-                c0 = c0 + n
+        def gelu(i):
+            gates[i] = keep.tile([P, pieces[i][2]], F32, name=f"gate{i}")
+            nc.scalar.activation(gates[i][:], sums[i, 0], GELU)
 
-        def finish(m, q, pieces=(256,)):
-            res = keep.tile([P, 256], F32, name=f"res{m}{q}")
-            c0 = 0
-            for n in pieces:
-                cols = slice(c0, c0 + n)
-                nc.vector.tensor_tensor(res[:, cols], gates[m, q][:, cols], sums[m, q, 1][:, cols], MULT)
-                nc.sync.dma_start(out[m * M_TILE : (m + 1) * M_TILE, q * 256 + c0 : q * 256 + c0 + n], res[:, cols])
-                c0 = c0 + n
+        def finish(*group):
+            m, j0 = pieces[group[0]][:2]
+            res = keep.tile([P, sum(pieces[i][2] for i in group)], F32, name=f"res{group[0]}")
+            for i in group:
+                c0 = pieces[i][1] - j0
+                nc.vector.tensor_tensor(res[:, c0 : c0 + pieces[i][2]], gates[i][:], sums[i, 1], MULT)
+            nc.sync.dma_start(out[m * M_TILE : (m + 1) * M_TILE, j0 : j0 + res[:].shape[1]], res[:])
 
-        multiply(0, 0, 0, 0, 0)
-        multiply(0, 1, 0, 6, 0)
-        multiply(0, 0, 1, 1, 0)
-        multiply(0, 1, 1, 7, 0)
-        multiply(0, 2, 0, 2, 0)
-        multiply(1, 0, 0, 3, 0)
-        multiply(1, 1, 0, 3, 1)
-        multiply(0, 2, 1, 4, 0)
-        multiply(1, 2, 0, 5, 0)
-        for q in range(3):
-            gelu(0, q)
-        finish(0, 0)
+        multiply(0, 0, 5, 256)
+        multiply(1, 0, 0, 0)
+        multiply(2, 0, 6, 0)
+        multiply(0, 1, 1, 0)
+        multiply(1, 1, 1, 128)
+        multiply(2, 1, 7, 0)
+        multiply(3, 0, 2, 0)
+        multiply(4, 0, 3, 0)
+        multiply(5, 0, 3, 256)
+        multiply(3, 1, 4, 0)
+        for i in range(4):
+            gelu(i)
+        multiply(6, 0, 5, 0)
         finish(0, 1)
-        multiply(1, 0, 1, 0, 0)
-        multiply(1, 1, 1, 0, 1)
-        multiply(1, 2, 1, 1, 0)
-        multiply(0, 3, 0, 6, 0)
-        multiply(1, 3, 0, 2, 0)
-        multiply(0, 3, 1, 7, 0)
-        multiply(1, 3, 1, 7, 1)
-        for q in range(3):
-            gelu(1, q)
-        gelu(0, 3)
-        gelu(1, 3, (128, 128))
-        finish(0, 2)
-        for q in range(3):
-            finish(1, q)
-        finish(0, 3)
-        finish(1, 3, (128, 128))
+        finish(2)
+        multiply(4, 1, 0, 0)
+        multiply(5, 1, 0, 256)
+        multiply(6, 1, 1, 0)
+        multiply(7, 0, 6, 0)
+        multiply(8, 0, 2, 0)
+        multiply(9, 0, 2, 128)
+        multiply(7, 1, 7, 0)
+        multiply(8, 1, 7, 256)
+        multiply(9, 1, 7, 384)
+        for i in range(4, 10):
+            gelu(i)
+        for i in range(3, 10):
+            finish(i)

@@ -18,8 +18,28 @@ ADD = mybir.AluOpType.add
 
 P = 128
 PACK = 4
+GROUP = 16
+BLOCK = 8
+QUADRANT = 32
 M_TILE = 128
-N_TILE = 512
+BANK = 512
+QUARTER = S // 4
+GATE, VALUE = 0, 1
+
+PLANE_SPANS = ((0, 3 * QUARTER), (3 * QUARTER, QUARTER))
+
+PIECES = (
+    (0, 0, QUARTER // 2),
+    (0, QUARTER // 2, QUARTER // 2),
+    (0, QUARTER, QUARTER),
+    (0, 2 * QUARTER, QUARTER),
+    (1, 0, QUARTER),
+    (1, QUARTER, QUARTER),
+    (1, 2 * QUARTER, QUARTER),
+    (0, 3 * QUARTER, QUARTER),
+    (1, 3 * QUARTER, QUARTER // 2),
+    (1, 3 * QUARTER + QUARTER // 2, QUARTER // 2),
+)
 
 
 def tile_picked_phglu_gelu_p_kernel(tc, x_words, x_scales, w1, w2, offs, out):
@@ -28,54 +48,58 @@ def tile_picked_phglu_gelu_p_kernel(tc, x_words, x_scales, w1, w2, offs, out):
         keep = ctx.enter_context(tc.tile_pool(name="keep", bufs=1))
         psum = ctx.enter_context(tc.psum_pool(name="psum", bufs=1))
 
-        offsets = keep.tile([P, S // 16], U16, name="offsets")
+        offsets = keep.tile([P, S // GROUP], U16, name="offsets")
         nc.sync.dma_start(offsets[:], offs)
 
         scale_table = keep.tile([P, T], U8, name="scale_table", align_bytes=64)
         nc.vector.memset(scale_table[:].bitcast(I32), 0)
-        plane_spans = ((0, 768), (768, 256))
-        planes = [keep.tile([P, width], U8, name=f"x_plane{j0}", align_bytes=64) for j0, width in plane_spans]
+        planes = [keep.tile([P, width], U8, name=f"x_plane{j0}", align_bytes=64) for j0, width in PLANE_SPANS]
         for plane in planes:
             nc.vector.memset(plane[:].bitcast(I32), 0)
-        w_words = keep.tile([P, 4 * M_TILE], U32, name="w_words", align_bytes=64)
-        w_plane = keep.tile([P, 4 * M_TILE], U8, name="w_plane", align_bytes=64)
+
+        w_words = keep.tile([P, 2 * N], U32, name="w_words", align_bytes=64)
+        w_plane = keep.tile([P, 2 * N], U8, name="w_plane", align_bytes=64)
         nc.vector.memset(w_words[:].bitcast(I32), 0)
         nc.vector.memset(w_plane[:].bitcast(I32), 0)
-        word_table = keep.tile([P, T], U32, name="word_table", tag="word_table", align_bytes=64)
+
+        word_table = keep.tile([P, T], U32, name="word_table", align_bytes=64)
         raw = {}
 
-        def load_w(m, a):
-            t = keep.tile([P, PACK, M_TILE], F32, name=f"raw{m}{a}", tag=f"raw{m}{a}", align_bytes=64)
-            nc.sync.dma_start(t[:], (w1, w2)[a][:, m * M_TILE : (m + 1) * M_TILE].rearrange("(p j) c -> p j c", j=PACK))
-            raw[m, a] = t[:]
+        def load_w1(m):
+            rows = keep.tile([P, PACK, M_TILE], F32, name=f"w1_raw{m}", tag=f"w1_raw{m}", align_bytes=64)
+            nc.sync.dma_start(rows[:], w1[:, m * M_TILE : (m + 1) * M_TILE].rearrange("(p j) c -> p j c", j=PACK))
+            raw[m, GATE] = rows[:]
 
         words = x_words[0].rearrange("p c r -> p (c r)").bitcast(I32)
-        load_w(0, 0)
-        nc.sync.dma_start(scale_table[0:P:8, :].bitcast(I32), x_scales[0].bitcast(I32))
+        load_w1(0)
+        nc.sync.dma_start(scale_table[0:P:BLOCK, :].bitcast(I32), x_scales[0].bitcast(I32))
         for c0 in range(0, T, T // 2):
             nc.sync.dma_start(word_table[:, c0 : c0 + T // 2].bitcast(I32), words[:, c0 : c0 + T // 2])
-        w2_rows = keep.tile([P, PACK, N], F32, name="w2_rows", align_bytes=64)
-        nc.sync.dma_start(w2_rows[:], w2.rearrange("(p j) c -> p j c", j=PACK))
+        w2_raw = keep.tile([P, PACK, N], F32, name="w2_raw", align_bytes=64)
+        nc.sync.dma_start(w2_raw[:], w2.rearrange("(p j) c -> p j c", j=PACK))
         for m in range(2):
-            raw[m, 1] = w2_rows[:, :, m * M_TILE : (m + 1) * M_TILE]
-        load_w(1, 0)
+            raw[m, VALUE] = w2_raw[:, :, m * M_TILE : (m + 1) * M_TILE]
+        load_w1(1)
 
-        warm = keep.tile([P, 2], F32, name="warm")
-        nc.gpsimd.memset(warm[:, 0:1], 0.0)
-        nc.scalar.activation(warm[:, 1:2], warm[:, 0:1], GELU)
+        warm = keep.tile([P, 1], F32, name="warm")
+        nc.scalar.activation(warm[:], w_words[:, 0:1].bitcast(F32), GELU)
 
-        for plane, (j0, width) in zip(planes, plane_spans):
+        for plane, (j0, width) in zip(planes, PLANE_SPANS):
             picked_scales = keep.tile([P, width], U8, name=f"picked_scales{j0}", align_bytes=64)
-            nc.vector.tensor_copy(picked_scales[:], scale_table[:].indirect(offsets[:, j0 // 16 : (j0 + width) // 16]))
-            for i in range(4):
+            nc.vector.tensor_copy(
+                picked_scales[:], scale_table[:].indirect(offsets[:, j0 // GROUP : (j0 + width) // GROUP])
+            )
+            for i in range(QUADRANT // BLOCK):
                 queue = nc.scalar if j0 == 0 and i % 2 else nc.sync
-                queue.dma_start(plane[i:P:32, :].bitcast(I32), picked_scales[8 * i : P : 32, :].bitcast(I32))
+                queue.dma_start(
+                    plane[i:P:QUADRANT, :].bitcast(I32), picked_scales[BLOCK * i : P : QUADRANT, :].bitcast(I32)
+                )
 
         codes = {}
 
         def quantize_w(m, a):
-            grouped = keep.tile([P, M_TILE, PACK], BF16, name=f"grouped{m}{a}", tag=f"grouped{m}{a}", align_bytes=64)
-            if (m, a) == (1, 1):
+            grouped = keep.tile([P, M_TILE, PACK], BF16, name=f"grouped{m}{a}", align_bytes=64)
+            if (m, a) == (1, VALUE):
                 nc.gpsimd.tensor_scalar(
                     out=grouped[:], in0=raw[m, a].rearrange("p j c -> p c j"), scalar1=1.0, scalar2=0.0, op0=MULT, op1=ADD
                 )
@@ -83,108 +107,97 @@ def tile_picked_phglu_gelu_p_kernel(tc, x_words, x_scales, w1, w2, offs, out):
                 nc.scalar.copy(
                     grouped[:].rearrange("p (c i) j -> p c j i", i=4), raw[m, a].rearrange("p j (c i) -> p c j i", i=4)
                 )
-            cols = slice((2 * a + m) * M_TILE, (2 * a + m + 1) * M_TILE)
+            cols = slice(a * N + m * M_TILE, a * N + (m + 1) * M_TILE)
             nc.vector.quantize_mx(
                 out=w_words[:, cols].bitcast(FP8X4), scales=w_plane[:, cols], in_=grouped[:].rearrange("p c j -> p (c j)")
             )
             codes[m, a] = (w_words[:, cols].bitcast(FP8X4), w_plane[:, cols])
 
-        banks = [psum.tile([P, N_TILE], F32, name=f"bank{b}") for b in range(8)]
+        banks = [psum.tile([P, BANK], F32, name=f"bank{b}") for b in range(8)]
 
-        quantize_w(0, 0)
+        quantize_w(0, GATE)
         for bank in banks[6:]:
             nc.tensor.matmul_mx(
                 out=bank[:],
-                lhsT=codes[0, 0][0],
-                lhsT_scale=codes[0, 0][1],
+                lhsT=codes[0, GATE][0],
+                lhsT_scale=codes[0, GATE][1],
                 rhs=w_words[:].bitcast(FP8X4),
                 rhs_scale=w_plane[:],
                 start=True,
                 stop=True,
             )
 
-        picked = {}
+        picked_words = {}
 
-        def gather(j0, width, tag):
-            t = keep.tile([P, width], U32, name=f"picked{j0}", tag=tag, align_bytes=64)
-            nc.vector.tensor_copy(t[:], word_table[:].indirect(offsets[:, j0 // 16 : (j0 + width) // 16]))
-            for c0 in range(0, width, 256):
-                picked[(j0 + c0) // 256] = t[:, c0 : c0 + 256]
+        def gather_words(j0, width, tag):
+            gathered = keep.tile([P, width], U32, name=f"picked_words{j0}", tag=tag, align_bytes=64)
+            nc.vector.tensor_copy(gathered[:], word_table[:].indirect(offsets[:, j0 // GROUP : (j0 + width) // GROUP]))
+            for c0 in range(0, width, QUARTER):
+                picked_words[(j0 + c0) // QUARTER] = gathered[:, c0 : c0 + QUARTER]
 
-        gather(0, 512, "picked0")
-        gather(512, 256, "picked512")
-        quantize_w(0, 1)
-        quantize_w(1, 1)
-        quantize_w(1, 0)
-        gather(768, 256, "raw10")
+        gather_words(0, 2 * QUARTER, "picked_half")
+        gather_words(2 * QUARTER, QUARTER, "picked_quarter")
+        quantize_w(0, VALUE)
+        quantize_w(1, VALUE)
+        quantize_w(1, GATE)
+        gather_words(3 * QUARTER, QUARTER, "w1_raw1")
 
-        pieces = (
-            (0, 0, 128),
-            (0, 128, 128),
-            (0, 256, 256),
-            (0, 512, 256),
-            (1, 0, 256),
-            (1, 256, 256),
-            (1, 512, 256),
-            (0, 768, 256),
-            (1, 768, 128),
-            (1, 896, 128),
-        )
         sums = {}
         gates = {}
 
         def multiply(i, a, bank, c0):
-            m, j0, width = pieces[i]
-            h = 0 if j0 < plane_spans[1][0] else 1
-            p0 = j0 - plane_spans[h][0]
+            m, j0, width = PIECES[i]
+            h = 0 if j0 < PLANE_SPANS[1][0] else 1
+            p0 = j0 - PLANE_SPANS[h][0]
             sums[i, a] = banks[bank][:, c0 : c0 + width]
             nc.tensor.matmul_mx(
                 out=sums[i, a],
                 lhsT=codes[m, a][0],
                 lhsT_scale=codes[m, a][1],
-                rhs=picked[j0 // 256][:, j0 % 256 : j0 % 256 + width].bitcast(FP8X4),
+                rhs=picked_words[j0 // QUARTER][:, j0 % QUARTER : j0 % QUARTER + width].bitcast(FP8X4),
                 rhs_scale=planes[h][:, p0 : p0 + width],
                 start=True,
                 stop=True,
             )
 
         def gelu(i):
-            gates[i] = keep.tile([P, pieces[i][2]], F32, name=f"gate{i}")
-            nc.scalar.activation(gates[i][:], sums[i, 0], GELU)
+            gates[i] = keep.tile([P, PIECES[i][2]], F32, name=f"gate{i}")
+            nc.scalar.activation(gates[i][:], sums[i, GATE], GELU)
 
         def finish(*group):
-            m, j0 = pieces[group[0]][:2]
-            res = keep.tile([P, sum(pieces[i][2] for i in group)], F32, name=f"res{group[0]}")
+            m, j0 = PIECES[group[0]][:2]
+            total = sum(PIECES[i][2] for i in group)
+            result = keep.tile([P, total], F32, name=f"result{group[0]}")
             for i in group:
-                c0 = pieces[i][1] - j0
-                nc.vector.tensor_tensor(res[:, c0 : c0 + pieces[i][2]], gates[i][:], sums[i, 1], MULT)
-            nc.sync.dma_start(out[m * M_TILE : (m + 1) * M_TILE, j0 : j0 + res[:].shape[1]], res[:])
+                c0 = PIECES[i][1] - j0
+                nc.vector.tensor_tensor(result[:, c0 : c0 + PIECES[i][2]], gates[i][:], sums[i, VALUE], MULT)
+            nc.sync.dma_start(out[m * M_TILE : (m + 1) * M_TILE, j0 : j0 + total], result[:])
 
-        multiply(0, 0, 5, 256)
-        multiply(1, 0, 0, 0)
-        multiply(2, 0, 6, 0)
-        multiply(0, 1, 1, 0)
-        multiply(1, 1, 1, 128)
-        multiply(2, 1, 7, 0)
-        multiply(3, 0, 2, 0)
-        multiply(4, 0, 3, 0)
-        multiply(5, 0, 3, 256)
-        multiply(3, 1, 4, 0)
+        multiply(0, GATE, 5, QUARTER)
+        multiply(1, GATE, 0, 0)
+        multiply(2, GATE, 6, 0)
+        multiply(0, VALUE, 1, 0)
+        multiply(1, VALUE, 1, QUARTER // 2)
+        multiply(2, VALUE, 7, 0)
+        multiply(3, GATE, 2, 0)
+        multiply(4, GATE, 3, 0)
+        multiply(5, GATE, 3, QUARTER)
+        multiply(3, VALUE, 4, 0)
         for i in range(4):
             gelu(i)
-        multiply(6, 0, 5, 0)
+        multiply(6, GATE, 5, 0)
         finish(0, 1)
         finish(2)
-        multiply(4, 1, 0, 0)
-        multiply(5, 1, 0, 256)
-        multiply(6, 1, 1, 0)
-        multiply(7, 0, 6, 0)
-        multiply(8, 0, 2, 0)
-        multiply(9, 0, 2, 128)
-        multiply(7, 1, 7, 0)
-        multiply(8, 1, 7, 256)
-        multiply(9, 1, 7, 384)
-        for i in range(4, 10):
+        multiply(4, VALUE, 0, 0)
+        multiply(5, VALUE, 0, QUARTER)
+        multiply(6, VALUE, 1, 0)
+        multiply(7, GATE, 6, 0)
+        multiply(8, GATE, 2, 0)
+        multiply(9, GATE, 2, QUARTER // 2)
+        multiply(7, VALUE, 7, 0)
+        multiply(8, VALUE, 7, QUARTER)
+        multiply(9, VALUE, 7, QUARTER + QUARTER // 2)
+        for i in range(4, len(PIECES)):
             gelu(i)
-        for i in range(3, 10):
+        for i in range(3, len(PIECES)):
             finish(i)

@@ -57,10 +57,9 @@ def tile_picked_phglu_gelu_p_kernel(tc, x_words, x_scales, w1, w2, offs, out):
         for plane in planes:
             nc.vector.memset(plane[:].bitcast(I32), 0)
 
-        w_words = keep.tile([P, 2 * N], U32, name="w_words", align_bytes=64)
+        w_words = keep.tile([P, M_TILE + BANK], U32, name="w_words", align_bytes=64)
         w_plane = keep.tile([P, 2 * N], U8, name="w_plane", align_bytes=64)
-        nc.vector.memset(w_words[:].bitcast(I32), 0)
-        nc.vector.memset(w_plane[:].bitcast(I32), 0)
+        nc.vector.memset(w_words[:, M_TILE:].bitcast(I32), 0)
 
         word_table = keep.tile([P, T], U32, name="word_table", align_bytes=64)
         raw = {}
@@ -82,15 +81,17 @@ def tile_picked_phglu_gelu_p_kernel(tc, x_words, x_scales, w1, w2, offs, out):
         load_w1(1)
 
         warm = keep.tile([P, 1], F32, name="warm")
-        nc.scalar.activation(warm[:], w_words[:, 0:1].bitcast(F32), GELU)
+        nc.scalar.activation(warm[:], w_words[:, BANK : BANK + 1].bitcast(F32), GELU)
 
+        picked = []
         for plane, (j0, width) in zip(planes, PLANE_SPANS):
-            picked_scales = keep.tile([P, width], U8, name=f"picked_scales{j0}", align_bytes=64)
+            picked_scales = keep.tile([P, width], U8, name=f"picked_scales{j0}", tag=f"picked_scales{j0}", align_bytes=64)
+            picked.append(picked_scales)
             nc.vector.tensor_copy(
                 picked_scales[:], scale_table[:].indirect(offsets[:, j0 // GROUP : (j0 + width) // GROUP])
             )
             for i in range(QUADRANT // BLOCK):
-                queue = nc.scalar if j0 == 0 and i % 2 else nc.sync
+                queue = nc.scalar if j0 == 0 else nc.sync
                 queue.dma_start(
                     plane[i:P:QUADRANT, :].bitcast(I32), picked_scales[BLOCK * i : P : QUADRANT, :].bitcast(I32)
                 )
@@ -119,10 +120,10 @@ def tile_picked_phglu_gelu_p_kernel(tc, x_words, x_scales, w1, w2, offs, out):
         for bank in banks[6:]:
             nc.tensor.matmul_mx(
                 out=bank[:],
-                lhsT=codes[0, GATE][0],
-                lhsT_scale=codes[0, GATE][1],
-                rhs=w_words[:].bitcast(FP8X4),
-                rhs_scale=w_plane[:],
+                lhsT=w_words[:, BANK:].bitcast(FP8X4),
+                lhsT_scale=picked[1][:, :M_TILE],
+                rhs=w_words[:, M_TILE:].bitcast(FP8X4),
+                rhs_scale=picked[0][:, :BANK],
                 start=True,
                 stop=True,
             )
@@ -138,9 +139,9 @@ def tile_picked_phglu_gelu_p_kernel(tc, x_words, x_scales, w1, w2, offs, out):
         gather_words(0, 2 * QUARTER, "picked_half")
         gather_words(2 * QUARTER, QUARTER, "picked_quarter")
         quantize_w(0, VALUE)
-        quantize_w(1, VALUE)
+        gather_words(3 * QUARTER, QUARTER, "picked_scales0")
         quantize_w(1, GATE)
-        gather_words(3 * QUARTER, QUARTER, "w1_raw1")
+        quantize_w(1, VALUE)
 
         sums = {}
         gates = {}
@@ -180,9 +181,9 @@ def tile_picked_phglu_gelu_p_kernel(tc, x_words, x_scales, w1, w2, offs, out):
         multiply(1, VALUE, 1, QUARTER // 2)
         multiply(2, VALUE, 7, 0)
         multiply(3, GATE, 2, 0)
+        multiply(3, VALUE, 4, 0)
         multiply(4, GATE, 3, 0)
         multiply(5, GATE, 3, QUARTER)
-        multiply(3, VALUE, 4, 0)
         for i in range(4):
             gelu(i)
         multiply(6, GATE, 5, 0)

@@ -49,7 +49,6 @@ def tile_picked_phglu_gelu_p_kernel(tc, x_words, x_scales, w1, w2, offs, out):
         psum = ctx.enter_context(tc.psum_pool(name="psum", bufs=1))
 
         offsets = keep.tile([P, S // GROUP], U16, name="offsets")
-        nc.sync.dma_start(offsets[:], offs)
 
         scale_table = keep.tile([P, T], U8, name="scale_table", align_bytes=64)
         nc.vector.memset(scale_table[:].bitcast(I32), 0)
@@ -71,9 +70,9 @@ def tile_picked_phglu_gelu_p_kernel(tc, x_words, x_scales, w1, w2, offs, out):
 
         words = x_words[0].rearrange("p c r -> p (c r)").bitcast(I32)
         load_w1(0)
+        nc.sync.dma_start(offsets[:], offs)
         nc.sync.dma_start(scale_table[0:P:BLOCK, :].bitcast(I32), x_scales[0].bitcast(I32))
-        for c0 in range(0, T, T // 2):
-            nc.sync.dma_start(word_table[:, c0 : c0 + T // 2].bitcast(I32), words[:, c0 : c0 + T // 2])
+        nc.sync.dma_start(word_table[:].bitcast(I32), words)
         w2_raw = keep.tile([P, PACK, N], F32, name="w2_raw", align_bytes=64)
         nc.sync.dma_start(w2_raw[:], w2.rearrange("(p j) c -> p j c", j=PACK))
         for m in range(2):
@@ -136,12 +135,11 @@ def tile_picked_phglu_gelu_p_kernel(tc, x_words, x_scales, w1, w2, offs, out):
             for c0 in range(0, width, QUARTER):
                 picked_words[(j0 + c0) // QUARTER] = gathered[:, c0 : c0 + QUARTER]
 
-        gather_words(0, 2 * QUARTER, "picked_half")
-        gather_words(2 * QUARTER, QUARTER, "picked_quarter")
+        gather_words(0, 2 * QUARTER, "picked_first")
+        gather_words(2 * QUARTER, 2 * QUARTER, "picked_second")
         quantize_w(0, VALUE)
-        gather_words(3 * QUARTER, QUARTER, "picked_scales0")
-        quantize_w(1, GATE)
         quantize_w(1, VALUE)
+        quantize_w(1, GATE)
 
         sums = {}
         gates = {}

@@ -64,15 +64,14 @@ def tile_picked_phglu_gelu_p_kernel(tc, x_words, x_scales, w1, w2, offs, out):
         raw = {}
 
         def load_w1(m):
-            rows = keep.tile([P, PACK, M_TILE], F32, name=f"w1_raw{m}", tag=f"w1_raw{m}", align_bytes=64)
+            rows = keep.tile([P, PACK, M_TILE], F32, name=f"w1_raw{m}", align_bytes=64)
             nc.sync.dma_start(rows[:], w1[:, m * M_TILE : (m + 1) * M_TILE].rearrange("(p j) c -> p j c", j=PACK))
             raw[m, GATE] = rows[:]
 
-        words = x_words[0].rearrange("p c r -> p (c r)").bitcast(I32)
         load_w1(0)
         nc.sync.dma_start(offsets[:], offs)
         nc.sync.dma_start(scale_table[0:P:BLOCK, :].bitcast(I32), x_scales[0].bitcast(I32))
-        nc.sync.dma_start(word_table[:].bitcast(I32), words)
+        nc.sync.dma_start(word_table[:].bitcast(I32), x_words[0].rearrange("p c r -> p (c r)").bitcast(I32))
         w2_raw = keep.tile([P, PACK, N], F32, name="w2_raw", align_bytes=64)
         nc.sync.dma_start(w2_raw[:], w2.rearrange("(p j) c -> p j c", j=PACK))
         for m in range(2):
@@ -82,18 +81,13 @@ def tile_picked_phglu_gelu_p_kernel(tc, x_words, x_scales, w1, w2, offs, out):
         warm = keep.tile([P, 1], F32, name="warm")
         nc.scalar.activation(warm[:], w_words[:, BANK : BANK + 1].bitcast(F32), GELU)
 
-        picked = []
-        for plane, (j0, width) in zip(planes, PLANE_SPANS):
-            picked_scales = keep.tile([P, width], U8, name=f"picked_scales{j0}", tag=f"picked_scales{j0}", align_bytes=64)
-            picked.append(picked_scales)
-            nc.vector.tensor_copy(
-                picked_scales[:], scale_table[:].indirect(offsets[:, j0 // GROUP : (j0 + width) // GROUP])
-            )
+        picked_scales = []
+        for plane, (j0, width), queue in zip(planes, PLANE_SPANS, (nc.scalar, nc.sync)):
+            picked = keep.tile([P, width], U8, name=f"picked_scales{j0}", tag=f"picked_scales{j0}", align_bytes=64)
+            picked_scales.append(picked)
+            nc.vector.tensor_copy(picked[:], scale_table[:].indirect(offsets[:, j0 // GROUP : (j0 + width) // GROUP]))
             for i in range(QUADRANT // BLOCK):
-                queue = nc.scalar if j0 == 0 else nc.sync
-                queue.dma_start(
-                    plane[i:P:QUADRANT, :].bitcast(I32), picked_scales[BLOCK * i : P : QUADRANT, :].bitcast(I32)
-                )
+                queue.dma_start(plane[i:P:QUADRANT, :].bitcast(I32), picked[BLOCK * i : P : QUADRANT, :].bitcast(I32))
 
         codes = {}
 
@@ -120,9 +114,9 @@ def tile_picked_phglu_gelu_p_kernel(tc, x_words, x_scales, w1, w2, offs, out):
             nc.tensor.matmul_mx(
                 out=bank[:],
                 lhsT=w_words[:, BANK:].bitcast(FP8X4),
-                lhsT_scale=picked[1][:, :M_TILE],
+                lhsT_scale=picked_scales[1][:, :M_TILE],
                 rhs=w_words[:, M_TILE:].bitcast(FP8X4),
-                rhs_scale=picked[0][:, :BANK],
+                rhs_scale=picked_scales[0][:, :BANK],
                 start=True,
                 stop=True,
             )
@@ -135,11 +129,12 @@ def tile_picked_phglu_gelu_p_kernel(tc, x_words, x_scales, w1, w2, offs, out):
             for c0 in range(0, width, QUARTER):
                 picked_words[(j0 + c0) // QUARTER] = gathered[:, c0 : c0 + QUARTER]
 
-        gather_words(0, 2 * QUARTER, "picked_first")
-        gather_words(2 * QUARTER, 2 * QUARTER, "picked_second")
+        gather_words(0, 2 * QUARTER, "picked_half")
+        gather_words(2 * QUARTER, QUARTER, "picked_quarter")
         quantize_w(0, VALUE)
-        quantize_w(1, VALUE)
+        gather_words(3 * QUARTER, QUARTER, "picked_scales0")
         quantize_w(1, GATE)
+        quantize_w(1, VALUE)
 
         sums = {}
         gates = {}

from contextlib import ExitStack

import concourse.mybir as mybir

K, T, S, N = 512, 2048, 1024, 256
FLOPS = 2 * 2 * K * N * S

F32 = mybir.dt.float32
BF16 = mybir.dt.bfloat16
I32 = mybir.dt.int32
U32 = mybir.dt.uint32
U16 = mybir.dt.uint16
U8 = mybir.dt.uint8
FP8X4 = mybir.dt.float8_e4m3fn_x4
GELU = mybir.ActivationFunctionType.Gelu_apprx_tanh
MULT = mybir.AluOpType.mult
ADD = mybir.AluOpType.add

P = 128
PACK = 4
GROUP = 16
BLOCK = 8
QUADRANT = 32
M_TILE = 128
BANK = 512
QUARTER = S // 4
GATE, VALUE = 0, 1

PLANE_SPANS = ((0, 3 * QUARTER), (3 * QUARTER, QUARTER))

PIECES = (
    (0, 0, QUARTER // 2),
    (0, QUARTER // 2, QUARTER // 2),
    (0, QUARTER, QUARTER),
    (0, 2 * QUARTER, QUARTER),
    (1, 0, QUARTER),
    (1, QUARTER, QUARTER),
    (1, 2 * QUARTER, QUARTER),
    (0, 3 * QUARTER, QUARTER),
    (1, 3 * QUARTER, QUARTER // 2),
    (1, 3 * QUARTER + QUARTER // 2, QUARTER // 2),
)


def tile_picked_phglu_gelu_p_kernel(tc, x_words, x_scales, w1, w2, offs, out):
    nc = tc.nc
    with ExitStack() as ctx:
        keep = ctx.enter_context(tc.tile_pool(name="keep", bufs=1))
        psum = ctx.enter_context(tc.psum_pool(name="psum", bufs=1))

        offsets = keep.tile([P, S // GROUP], U16, name="offsets")

        scale_table = keep.tile([P, T], U8, name="scale_table", align_bytes=64)
        nc.vector.memset(scale_table[:].bitcast(I32), 0)
        planes = [keep.tile([P, width], U8, name=f"x_plane{j0}", align_bytes=64) for j0, width in PLANE_SPANS]
        for plane in planes:
            nc.vector.memset(plane[:].bitcast(I32), 0)

        w_words = keep.tile([P, M_TILE + BANK], U32, name="w_words", align_bytes=64)
        w_plane = keep.tile([P, 2 * N], U8, name="w_plane", align_bytes=64)
        nc.vector.memset(w_words[:, M_TILE:].bitcast(I32), 0)

        word_table = keep.tile([P, T], U32, name="word_table", align_bytes=64)
        raw = {}

        def load_w1(m):
            rows = keep.tile([P, PACK, M_TILE], F32, name=f"w1_raw{m}", align_bytes=64)
            nc.sync.dma_start(rows[:], w1[:, m * M_TILE : (m + 1) * M_TILE].rearrange("(p j) c -> p j c", j=PACK))
            raw[m, GATE] = rows[:]

        load_w1(0)
        nc.sync.dma_start(offsets[:], offs)
        nc.sync.dma_start(scale_table[0:P:BLOCK, :].bitcast(I32), x_scales[0].bitcast(I32))
        nc.sync.dma_start(word_table[:].bitcast(I32), x_words[0].rearrange("p c r -> p (c r)").bitcast(I32))
        w2_raw = keep.tile([P, PACK, N], F32, name="w2_raw", align_bytes=64)
        nc.sync.dma_start(w2_raw[:], w2.rearrange("(p j) c -> p j c", j=PACK))
        for m in range(2):
            raw[m, VALUE] = w2_raw[:, :, m * M_TILE : (m + 1) * M_TILE]
        load_w1(1)

        warm = keep.tile([P, 1], F32, name="warm")
        nc.scalar.activation(warm[:], w_words[:, BANK : BANK + 1].bitcast(F32), GELU)

        picked_scales = []
        for plane, (j0, width), queue in zip(planes, PLANE_SPANS, (nc.scalar, nc.sync)):
            picked = keep.tile([P, width], U8, name=f"picked_scales{j0}", tag=f"picked_scales{j0}", align_bytes=64)
            picked_scales.append(picked)
            nc.vector.tensor_copy(picked[:], scale_table[:].indirect(offsets[:, j0 // GROUP : (j0 + width) // GROUP]))
            for i in range(QUADRANT // BLOCK):
                queue.dma_start(plane[i:P:QUADRANT, :].bitcast(I32), picked[BLOCK * i : P : QUADRANT, :].bitcast(I32))

        codes = {}

        def quantize_w(m, a):
            grouped = keep.tile([P, M_TILE, PACK], BF16, name=f"grouped{m}{a}", align_bytes=64)
            if (m, a) == (1, VALUE):
                nc.gpsimd.tensor_scalar(
                    out=grouped[:], in0=raw[m, a].rearrange("p j c -> p c j"), scalar1=1.0, scalar2=0.0, op0=MULT, op1=ADD
                )
            else:
                nc.scalar.copy(
                    grouped[:].rearrange("p (c i) j -> p c j i", i=4), raw[m, a].rearrange("p j (c i) -> p c j i", i=4)
                )
            cols = slice(a * N + m * M_TILE, a * N + (m + 1) * M_TILE)
            nc.vector.quantize_mx(
                out=w_words[:, cols].bitcast(FP8X4), scales=w_plane[:, cols], in_=grouped[:].rearrange("p c j -> p (c j)")
            )
            codes[m, a] = (w_words[:, cols].bitcast(FP8X4), w_plane[:, cols])

        banks = [psum.tile([P, BANK], F32, name=f"bank{b}") for b in range(8)]

        quantize_w(0, GATE)
        for bank in banks[6:]:
            nc.tensor.matmul_mx(
                out=bank[:],
                lhsT=w_words[:, BANK:].bitcast(FP8X4),
                lhsT_scale=picked_scales[1][:, :M_TILE],
                rhs=w_words[:, M_TILE:].bitcast(FP8X4),
                rhs_scale=picked_scales[0][:, :BANK],
                start=True,
                stop=True,
            )

        picked_words = {}

        def gather_words(j0, width, tag):
            gathered = keep.tile([P, width], U32, name=f"picked_words{j0}", tag=tag, align_bytes=64)
            nc.vector.tensor_copy(gathered[:], word_table[:].indirect(offsets[:, j0 // GROUP : (j0 + width) // GROUP]))
            for c0 in range(0, width, QUARTER):
                picked_words[(j0 + c0) // QUARTER] = gathered[:, c0 : c0 + QUARTER]

        gather_words(0, 2 * QUARTER, "picked_half")
        gather_words(2 * QUARTER, QUARTER, "picked_quarter")
        quantize_w(0, VALUE)
        gather_words(3 * QUARTER, QUARTER, "picked_scales0")
        quantize_w(1, GATE)
        quantize_w(1, VALUE)

        sums = {}
        gates = {}

        def multiply(i, a, bank, c0):
            m, j0, width = PIECES[i]
            h = 0 if j0 < PLANE_SPANS[1][0] else 1
            p0 = j0 - PLANE_SPANS[h][0]
            sums[i, a] = banks[bank][:, c0 : c0 + width]
            nc.tensor.matmul_mx(
                out=sums[i, a],
                lhsT=codes[m, a][0],
                lhsT_scale=codes[m, a][1],
                rhs=picked_words[j0 // QUARTER][:, j0 % QUARTER : j0 % QUARTER + width].bitcast(FP8X4),
                rhs_scale=planes[h][:, p0 : p0 + width],
                start=True,
                stop=True,
            )

        def gelu(i):
            gates[i] = keep.tile([P, PIECES[i][2]], F32, name=f"gate{i}")
            nc.scalar.activation(gates[i][:], sums[i, GATE], GELU)

        def finish(*group):
            m, j0 = PIECES[group[0]][:2]
            total = sum(PIECES[i][2] for i in group)
            result = keep.tile([P, total], F32, name=f"result{group[0]}")
            for i in group:
                c0 = PIECES[i][1] - j0
                nc.vector.tensor_tensor(result[:, c0 : c0 + PIECES[i][2]], gates[i][:], sums[i, VALUE], MULT)
            nc.sync.dma_start(out[m * M_TILE : (m + 1) * M_TILE, j0 : j0 + total], result[:])

        multiply(0, GATE, 5, QUARTER)
        multiply(1, GATE, 0, 0)
        multiply(2, GATE, 6, 0)
        multiply(0, VALUE, 1, 0)
        multiply(1, VALUE, 1, QUARTER // 2)
        multiply(2, VALUE, 7, 0)
        multiply(3, GATE, 2, 0)
        multiply(3, VALUE, 4, 0)
        multiply(4, GATE, 3, 0)
        multiply(5, GATE, 3, QUARTER)
        for i in range(4):
            gelu(i)
        multiply(6, GATE, 5, 0)
        finish(0, 1)
        finish(2)
        multiply(4, VALUE, 0, 0)
        multiply(5, VALUE, 0, QUARTER)
        multiply(6, VALUE, 1, 0)
        multiply(7, GATE, 6, 0)
        multiply(8, GATE, 2, 0)
        multiply(9, GATE, 2, QUARTER // 2)
        multiply(7, VALUE, 7, 0)
        multiply(8, VALUE, 7, QUARTER)
        multiply(9, VALUE, 7, QUARTER + QUARTER // 2)
        for i in range(4, len(PIECES)):
            gelu(i)
        for i in range(3, len(PIECES)):
            finish(i)
